import numpy as np
import ml_dtypes


def mxq(x, axis, fmt="e4m3"):
    dtype, down = {"e4m3": (ml_dtypes.float8_e4m3fn, 7), "e5m2": (ml_dtypes.float8_e5m2, 14)}[fmt]
    v = np.moveaxis(np.asarray(x, np.float32).astype(ml_dtypes.bfloat16).astype(np.float64), axis, -1)
    blocks = v.reshape(v.shape[:-1] + (-1, 32))
    amax = np.abs(blocks).max(-1, keepdims=True)
    byte = np.maximum(np.where(amax > 0, np.frexp(amax)[1] - 1 + 127, 0) - down, 1)
    scale = np.exp2(byte - 127.0)
    codes = (blocks / scale).astype(np.float32).astype(dtype).astype(np.float64)
    return np.moveaxis((codes * scale).reshape(v.shape), -1, axis)


WIDE = False


def mx_kscale(k):
    if not WIDE:
        return np.ones(k)
    levels = np.array([10, -10, 5, -5, 0])
    if k % 512:
        return np.exp2(np.random.permutation(np.resize(levels, k // 32))).repeat(32)
    a = np.empty((k // 512, 16))
    for p in range(k // 512):
        a[p, :8] = np.random.permutation(np.resize(levels, 8))
        for g in range(8):
            far = levels[np.abs(levels - a[p, g]) >= 10]
            a[p, g + 8] = far[np.random.randint(len(far))]
    return np.exp2(a.ravel()).repeat(32)


BF16 = ml_dtypes.bfloat16


def bf(x):
    return np.asarray(x, np.float32).astype(BF16)


def f64(x):
    return np.asarray(x).astype(np.float64)


T, D, I, J, O = 1024, 512, 4, 4, 128
M = I * J + I * J + I


def logsumexp(c, axis):
    m = c.max(axis=axis, keepdims=True)
    return m + np.log(np.sum(np.exp(c - m), axis=axis, keepdims=True))


def softmax(c, axis):
    e = np.exp(c - c.max(axis=axis, keepdims=True))
    return e / np.sum(e, axis=axis, keepdims=True)


def project(x, g, w):
    d, m, o = w.shape
    p = mxq(x * g[None, :], 1, "e4m3") @ mxq(w.reshape(d, m * o), 0, "e4m3")
    return p.reshape(x.shape[0], m, o)


def draw0():
    kd = mx_kscale(D)
    kt = mx_kscale(T)
    return {
        "x": bf(np.random.standard_normal((T, D))),
        "g": bf((1.0 + 0.1 * np.random.standard_normal(D)) * kd),
        "w": bf(np.random.standard_normal((D, M, O)) / np.sqrt(D) / kd[:, None, None]),
        "y": bf(np.random.standard_normal((T, O)) * 1.2),
        "s": bf(np.random.standard_normal((I, J, O)) * 0.4),
        "u": bf((1.0 + 0.1 * np.random.standard_normal(T)) / kt),
        "q": bf((1.0 + 0.1 * np.random.standard_normal(T)) * kt),
    }


def core(x, g, w, y, s, u, q):
    x, g, w, y, s, u, q = f64(x), f64(g), f64(w), f64(y), f64(s), f64(u), f64(q)
    t, d = x.shape
    ni, nj, o = s.shape
    n = ni * nj

    p = project(x, g, w)

    mu = p[:, :n].reshape(t, ni, nj, o)
    c = p[:, n:n + n].reshape(t, ni, nj, o)
    a = p[:, n + n:]

    lg2 = c - logsumexp(c, 2)

    r = y[:, None, None, :] - mu
    v = np.exp(-s)[None]
    joint = a[:, :, None, :] + lg2 - 0.5 * (s[None] + r ** 2 * v)

    h = softmax(joint, (1, 2))
    gm = h * r * v * q[:, None, None, None]

    xu = x * u[:, None]
    dw = (mxq(np.transpose(xu), 1, "e4m3") @ mxq(gm.reshape(t, n * o), 0, "e4m3")) / 8.0
    return dw.reshape(d, ni, nj, o)


def e4m3fn_bytes(y):
    return np.clip(np.asarray(y, np.float64), -448.0, 448.0).astype(np.float32).astype(ml_dtypes.float8_e4m3fn).view(np.uint8)


def e4m3fn_values(b):
    return np.asarray(b, np.uint8).view(ml_dtypes.float8_e4m3fn).astype(np.float64)


def setup_inputs():
    d = draw0()
    x0 = np.asarray(d['w']).astype(np.float64)
    s = (np.max(np.abs(x0), axis=(1, 2), keepdims=True) / 448.0).astype(np.float32)
    out = {}
    for k, v in d.items():
        if k == 'w':
            out['w_bytes'] = e4m3fn_bytes(x0 / s.astype(np.float64))
            out['w_scale'] = s
        else:
            out[k] = v
    return out


def reference(x, g, w_bytes, w_scale, y, s, u, q):
    return core(x, g, e4m3fn_values(w_bytes) * w_scale.astype(np.float64), y, s, u, q)

@@ -1,0 +1,565 @@
+import math
+from contextlib import ExitStack
+
+import concourse.mybir as mybir
+from concourse.masks import make_identity
+
+T, D, NI, NJ, O = 1024, 512, 4, 4, 128
+FLOPS = 2 * T * D * 36 * O + 2 * D * T * NI * NJ * O
+
+F32 = mybir.dt.float32
+BF16 = mybir.dt.bfloat16
+U32 = mybir.dt.uint32
+U8 = mybir.dt.uint8
+FP8 = mybir.dt.float8_e4m3fn
+X4 = mybir.dt.float8_e4m3fn_x4
+ALU = mybir.AluOpType
+ACT = mybir.ActivationFunctionType
+
+P = 128
+PACK = 4
+KP = P * PACK
+NG = T // KP
+OC = P // NI
+NC = O // OC
+UNITS = NC * NG
+BANKS = 8
+
+
+def tile_hierarchicalmixtureeffectiveweightgradie_kernel(tc, x, g, w_bytes, w_scale, y, s, u, q, out):
+    nc = tc.nc
+    with ExitStack() as ctx:
+        keep = ctx.enter_context(tc.tile_pool(name="keep", bufs=1))
+        work = ctx.enter_context(tc.tile_pool(name="work", bufs=1))
+        psum = ctx.enter_context(tc.psum_pool(name="psum", bufs=1))
+        ctx.enter_context(tc.manual_schedule())
+
+        free_banks = list(range(BANKS))
+        held = {}
+
+        def take(key, shape, dtype):
+            b = free_banks[0]
+            free_banks.remove(b)
+            bank = psum.tile(shape, dtype, name="bank%d" % b)
+            held[key] = (b, bank)
+            return bank
+
+        def give(key):
+            free_banks.append(held[key][0])
+
+        def at(key):
+            return held[key][1]
+
+        wrows = w_bytes.rearrange("(p t) m o -> p t m o", t=PACK)
+        ws = keep.tile([P, PACK], F32, name="ws")
+        nc.sync.dma_start(out=ws[:], in_=w_scale.rearrange("(p t) a b -> p (t a b)", t=PACK))
+        x_sb = [keep.tile([P, PACK, D], BF16, name="x_sb%d" % gi) for gi in range(NG)]
+        xrows = x.rearrange("(g p t) d -> g p t d", p=P, t=PACK)
+        wb_mu = [keep.tile([P, 2, 16 * O], U8, name="wb_mu%d" % h) for h in range(2)]
+        nc.sync.dma_start(out=wb_mu[0][:], in_=wrows[:, 0:2, 0:16, :].rearrange("p t m o -> p t (m o)"))
+        nc.sync.dma_start(out=x_sb[0][:], in_=xrows[0])
+        nc.sync.dma_start(out=wb_mu[1][:], in_=wrows[:, 2:4, 0:16, :].rearrange("p t m o -> p t (m o)"))
+        g4 = keep.tile([P, PACK], BF16, name="g4")
+        nc.sync.dma_start(out=g4[:], in_=g.rearrange("(p t) -> p t", t=PACK))
+        y_sb = keep.tile([P, NG, PACK, O], BF16, name="y_sb")
+        nc.sync.dma_start(out=y_sb[:], in_=y.rearrange("(g p t) o -> p g t o", p=P, t=PACK))
+        s_rows = keep.tile([P, P], BF16, name="s_rows")
+        nc.gpsimd.memset(s_rows[:], 0.0)
+        nc.sync.dma_start(out=s_rows[0:16, :].rearrange("r (i o) -> r i o", i=NI),
+                          in_=s.rearrange("i j (c o) -> (j c) i o", o=OC))
+        wb_c = keep.tile([P, PACK, 16 * O], U8, name="wb_c")
+        nc.sync.dma_start(out=wb_c[:], in_=wrows[:, :, 16:32, :].rearrange("p t m o -> p t (m o)"))
+        wb_a = keep.tile([P, PACK, NI * O], U8, name="wb_a")
+        nc.sync.dma_start(out=wb_a[:], in_=wrows[:, :, 32:36, :].rearrange("p t m o -> p t (m o)"))
+        nc.sync.dma_start(out=x_sb[1][:], in_=xrows[1])
+        q_sb = keep.tile([P, NG, PACK], BF16, name="q_sb")
+        nc.sync.dma_start(out=q_sb[:], in_=q.rearrange("(g p t) -> p g t", p=P, t=PACK))
+        u_sb = keep.tile([P, NG, PACK], BF16, name="u_sb")
+        nc.sync.dma_start(out=u_sb[:], in_=u.rearrange("(g p t) -> p g t", p=P, t=PACK))
+
+        ident = keep.tile([P, P], F32, name="ident")
+        make_identity(nc, ident[:])
+        ident_bf = keep.tile([P, P], BF16, name="ident_bf")
+        make_identity(nc, ident_bf[:])
+
+        wsn = keep.tile([P, PACK], F32, name="wsn")
+        wide_mu = keep.tile([P, PACK, NI, NJ, O], BF16, name="wide_mu")
+        wide_c = keep.tile([P, PACK, NI, NJ, O], BF16, name="wide_c")
+        wide_a = keep.tile([P, PACK, NI, 1, O], BF16, name="wide_a")
+
+        def widen(on_vector, wide, wb, scale, t):
+            dst = wide[:, t].rearrange("p i j o -> p (i j o)")
+            if on_vector:
+                nc.vector.tensor_scalar(out=dst, in0=wb.bitcast(FP8), scalar1=scale[:, t:t + 1], scalar2=None, op0=ALU.mult)
+            else:
+                nc.scalar.activation(out=dst, in_=wb.bitcast(FP8), func=ACT.Copy, scale=scale[:, t:t + 1])
+
+        wq = {}
+        grouped = {}
+        WIDTH = {"mu": 4, "c": 4, "a": 1}
+        SOURCE = {"mu": wide_mu, "c": wide_c, "a": wide_a}
+
+        def interleave(on_vector, c, kind, j):
+            if (c, kind) not in grouped:
+                grouped[(c, kind)] = work.tile([P, WIDTH[kind], NI, OC, PACK], BF16, name="grp_" + kind, align_bytes=64)
+            src = SOURCE[kind][:, :, :, j, c * OC:(c + 1) * OC]
+            if kind == "c" and j == 0:
+                if on_vector:
+                    nc.vector.tensor_scalar(out=grouped[(c, kind)][:, j], in0=src.rearrange("p t i o -> p i o t"),
+                                            scalar1=-1.0, scalar2=None, op0=ALU.mult)
+                else:
+                    nc.scalar.activation(out=grouped[(c, kind)][:, j], in_=src.rearrange("p t i o -> p i o t"),
+                                         func=ACT.Copy, scale=-1.0)
+                return
+            src = src.rearrange("p t i (a b) -> p i a t b", b=4)
+            dst = grouped[(c, kind)][:, j].rearrange("p i (a b) t -> p i a t b", b=4)
+            if on_vector:
+                nc.vector.tensor_copy(out=dst, in_=src)
+            else:
+                nc.scalar.copy(out=dst, in_=src)
+
+        def quantise(name, src, bufs):
+            n = src.shape[1] // PACK
+            codes = work.tile([P, n], U32, name=name + "_codes", bufs=bufs, align_bytes=64)
+            scales = work.tile([P, n], U8, name=name + "_scales", bufs=bufs, align_bytes=64)
+            nc.vector.quantize_mx(out=codes[:].bitcast(X4), scales=scales[:], in_=src)
+            return codes, scales
+
+        def quantise_w(c, kind):
+            wq[(c, kind)] = quantise("wq_" + kind, grouped[(c, kind)][:].rearrange("p j i o t -> p (j i o t)"), 2)
+
+        def mx(dst, lhs, l0, rhs, r0, n, start, stop):
+            nc.tensor.matmul_mx(out=dst, lhsT=lhs[0][:, l0:l0 + P].bitcast(X4), lhsT_scale=lhs[1][:, l0:l0 + P],
+                                rhs=rhs[0][:, r0:r0 + n].bitcast(X4), rhs_scale=rhs[1][:, r0:r0 + n], start=start, stop=stop)
+
+        xq = {}
+        xuq = {}
+        xg = {}
+
+        def turn_x(gi, half):
+            words = x_sb[gi][:].bitcast(F32)
+            bank = take(("xt", gi, half), [P, 2, 2, P], F32)
+            for tl in range(2):
+                for h in range(2):
+                    nc.tensor.transpose(bank[:, tl, h, :], words[:, 2 * half + tl, h::2], ident[:])
+
+        def gain_x(gi, half):
+            if gi not in xg:
+                xg[gi] = work.tile([P, PACK, P, 2, 2], BF16, name="xgrp", bufs=2, align_bytes=64)
+            bank = at(("xt", gi, half))
+            gb = g4[:].rearrange("p (h e) -> p h e", h=2).unsqueeze(1).broadcast_to([P, P, 2, 2])
+            for tl in range(2):
+                src = bank[:, tl].rearrange("p h n -> p (h n)").bitcast(BF16).rearrange("p (h n e) -> p n h e", h=2, e=2)
+                nc.vector.tensor_tensor(out=xg[gi][:, 2 * half + tl], in0=src, in1=gb, op=ALU.mult)
+            give(("xt", gi, half))
+
+        def quantise_xg(gi):
+            xq[gi] = quantise("xq", xg[gi][:].rearrange("p t n h e -> p (t n h e)"), NG)
+
+        xu = {}
+
+        def weigh_x(gi):
+            xu[gi] = work.tile([P, D, PACK], BF16, name="xgrp", bufs=2, align_bytes=64)
+            ub = u_sb[:, gi, :].unsqueeze(1).broadcast_to([P, D, PACK])
+            nc.vector.tensor_tensor(out=xu[gi][:], in0=x_sb[gi][:].rearrange("p t d -> p d t"), in1=ub, op=ALU.mult)
+
+        def quantise_xu(gi):
+            xuq[gi] = quantise("xuq", xu[gi][:].rearrange("p d t -> p (d t)"), NG)
+
+        yt = {}
+        yrep = {}
+
+        def spread_y(c):
+            yrep[c] = work.tile([P, NG * PACK, NI, OC], BF16, name="yrep")
+            src = y_sb[:].rearrange("p g t o -> p (g t) o")[:, :, c * OC:(c + 1) * OC].unsqueeze(2).broadcast_to([P, NG * PACK, NI, OC])
+            nc.vector.tensor_copy(out=yrep[c][:], in_=src)
+
+        def turn_y(c):
+            bank = take(("yt", c), [P, NG * PACK, P], BF16)
+            for n in range(NG * PACK):
+                nc.tensor.transpose(bank[:, n, :], yrep[c][:, n].rearrange("p i o -> p (i o)"), ident_bf[:])
+
+        def copy_y(c):
+            yt[c] = work.tile([P, NG, KP], BF16, name="yt", bufs=2)
+            nc.scalar.copy(out=yt[c][:].rearrange("p g n -> p (g n)"), in_=at(("yt", c))[:].rearrange("p n m -> p (n m)"))
+            give(("yt", c))
+
+        var = keep.tile([P, NJ * NC], F32, name="var")
+        root = keep.tile([P, NJ * NC], F32, name="root")
+        half_root = keep.tile([P, NJ * NC], F32, name="half_root")
+        half_s = keep.tile([P, NJ * NC], F32, name="half_s")
+
+        def variance_columns():
+            bank = take("st", [P, P], BF16)
+            nc.tensor.transpose(bank[:], s_rows[:], ident_bf[:])
+            nc.scalar.activation(out=var[:], in_=bank[:, 0:NJ * NC], func=ACT.Exp, scale=-1.0)
+            nc.scalar.activation(out=root[:], in_=bank[:, 0:NJ * NC], func=ACT.Exp, scale=-0.5)
+            nc.scalar.activation(out=half_s[:], in_=bank[:, 0:NJ * NC], func=ACT.Copy, scale=-0.5)
+            nc.scalar.activation(out=half_root[:], in_=root[:], func=ACT.Copy, scale=math.sqrt(0.5))
+            give("st")
+
+        def column(tile, k, j):
+            n = j * NC + k // NG
+            return tile[:, n:n + 1]
+
+        tiles = {}
+
+        def new(name, k, shape, dtype, bufs=1, align=32):
+            tiles[(name, k)] = work.tile(shape, dtype, name=name, bufs=bufs, align_bytes=align)
+            return tiles[(name, k)]
+
+        def get(name, k):
+            return tiles[(name, k)]
+
+        def turn_sum(dst, parts):
+            for n, part in enumerate(parts):
+                nc.tensor.matmul(dst, lhsT=part, rhs=ident[:], start=(n == 0), stop=(n == len(parts) - 1), is_transpose=True)
+
+        def block(tile, t):
+            return tile[:, t * P:(t + 1) * P]
+
+        def mu_mm(k, j):
+            bank = take(("mu", k, j), [P, KP], F32)
+            mx(bank[:], wq[(k // NG, "mu")], j * P, xq[k % NG], 0, KP, True, True)
+
+        def residual(k, j):
+            r = new("r%d" % j, k, [P, KP], F32, 2)
+            nc.vector.tensor_tensor(out=r[:], in0=yt[k // NG][:, k % NG], in1=at(("mu", k, j))[:], op=ALU.subtract)
+            give(("mu", k, j))
+
+        def square(k, j):
+            z2 = new("z2%d" % j, k, [P, KP], F32)
+            nc.scalar.activation(out=z2[:], in_=get("r%d" % j, k)[:], func=ACT.Square, scale=column(half_root, k, j))
+
+        def d_mm(k, j):
+            bank = take(("d", k, j), [P, KP], F32)
+            mx(bank[:], wq[(k // NG, "c")], j * P, xq[k % NG], 0, KP, True, False)
+            mx(bank[:], wq[(k // NG, "c")], 0, xq[k % NG], 0, KP, False, True)
+
+        def d1_copy(k):
+            nc.scalar.copy(out=new("d1", k, [P, KP], F32)[:], in_=at(("d", k, 1))[:])
+            give(("d", k, 1))
+
+        def max_a(k):
+            nc.vector.scalar_tensor_tensor(out=new("m12", k, [P, KP], F32)[:], in0=at(("d", k, 2))[:], scalar=0.0,
+                                           in1=get("d1", k)[:], op0=ALU.max, op1=ALU.max)
+
+        def max_b(k):
+            nc.vector.tensor_tensor(out=new("gap0", k, [P, KP], F32)[:], in0=at(("d", k, 3))[:], in1=get("m12", k)[:], op=ALU.max)
+
+        def gap_j(k, j):
+            src = get("d1", k) if j == 1 else at(("d", k, j))
+            nc.vector.tensor_tensor(out=new("gap%d" % j, k, [P, KP], F32)[:], in0=get("gap0", k)[:], in1=src[:], op=ALU.subtract)
+            if j != 1:
+                give(("d", k, j))
+
+        def exp_gap(k, j):
+            eg = new("eg%d" % j, k, [P, KP], F32)
+            nc.scalar.activation(out=eg[:], in_=get("gap%d" % j, k)[:], func=ACT.Exp, scale=-1.0)
+
+        def sum_j(key, name, k):
+            bank = take((key, k), [P, PACK, P], F32)
+            for t in range(PACK):
+                turn_sum(bank[:, t, :], [block(get(name + "%d" % j, k), t) for j in range(NJ)])
+
+        def s_copy(k):
+            nc.scalar.copy(out=new("S", k, [P, P, PACK], F32)[:], in_=at(("S", k))[:].rearrange("p t n -> p n t"))
+            give(("S", k))
+
+        def pair(k):
+            sv = get("S", k)[:].rearrange("p (h e o) t -> p h e (o t)", h=2, e=2)
+            nc.vector.tensor_tensor(out=new("pair", k, [P, 2, P], F32)[:], in0=sv[:, :, 0], in1=sv[:, :, 1], op=ALU.mult)
+
+        def cofactor(k):
+            sv = get("S", k)[:].rearrange("p (h e o) t -> p h e (o t)", h=2, e=2)
+            other = get("pair", k)[:, ::-1, :].unsqueeze(2).broadcast_to([P, 2, 2, P])
+            nc.vector.tensor_tensor(out=new("C", k, [P, 2, 2, P], F32, 2)[:], in0=sv[:, :, ::-1, :], in1=other, op=ALU.mult)
+
+        def cost_mm(k, j):
+            bank = take(("kn", k, j), [P, PACK, P], F32)
+            for t in range(PACK):
+                turn_sum(bank[:, t, :], [block(get("gap%d" % j, k), t), block(get("z2%d" % j, k), t)])
+
+        def cost_copy(k, j):
+            kn = new("kn%d" % j, k, [P, KP], F32)
+            nc.scalar.copy(out=kn[:], in_=at(("kn", k, j))[:].rearrange("p t n -> p (t n)"))
+            give(("kn", k, j))
+
+        def a_mm(k):
+            bank = take(("a", k), [P, PACK, P], F32)
+            for t in range(PACK):
+                mx(bank[:, t, :], xq[k % NG], t * P, wq[(k // NG, "a")], 0, P, True, True)
+
+        def a_copy(k):
+            nc.scalar.copy(out=new("na", k, [P, KP], F32)[:], in_=at(("a", k))[:].rearrange("p t n -> p (t n)"))
+            give(("a", k))
+
+        def min_pair(k, h):
+            n2 = new("n2", k, [P, 2, KP], F32) if h == 0 else get("n2", k)
+            nc.vector.tensor_tensor(out=n2[:, h], in0=get("kn%d" % h, k)[:], in1=get("kn%d" % (h + 2), k)[:], op=ALU.min)
+
+        def min_j(k):
+            n2 = get("n2", k)
+            nc.vector.tensor_tensor(out=new("n", k, [P, KP], F32)[:], in0=n2[:, 0], in1=n2[:, 1], op=ALU.min)
+
+        def add_a(k):
+            nc.vector.tensor_tensor(out=new("b", k, [P, KP], F32)[:], in0=get("n", k)[:], in1=get("na", k)[:], op=ALU.add)
+
+        def min_i_a(k):
+            b = get("b", k)[:].rearrange("p (t h n) -> p t h n", t=PACK, h=2)
+            nc.vector.tensor_tensor(out=new("b2", k, [P, PACK, 2 * OC], F32)[:], in0=b[:, :, 0], in1=b[:, :, 1], op=ALU.min)
+
+        def min_i_b(k):
+            b2 = get("b2", k)
+            nc.vector.tensor_tensor(out=new("low", k, [P, PACK, OC], F32)[:], in0=b2[:, :, 0:OC], in1=b2[:, :, OC:], op=ALU.min)
+
+        def shift(k):
+            low = get("low", k)[:].unsqueeze(2).broadcast_to([P, PACK, NI, OC])
+            sh = new("sh", k, [P, KP], F32)
+            nc.vector.tensor_tensor(out=sh[:].rearrange("p (t i o) -> p t i o", t=PACK, i=NI),
+                                    in0=get("na", k)[:].rearrange("p (t i o) -> p t i o", t=PACK, i=NI), in1=low, op=ALU.subtract)
+
+        def arg_mm(k, j):
+            bank = take(("arg", k, j), [P, PACK, P], F32)
+            for t in range(PACK):
+                turn_sum(bank[:, t, :], [block(get("kn%d" % j, k), t), block(get("sh", k), t)])
+
+        def exp_arg(k, j):
+            e = new("e%d" % j, k, [P, KP], F32)
+            nc.scalar.activation(out=e[:], in_=at(("arg", k, j))[:].rearrange("p t n -> p (t n)"), func=ACT.Exp,
+                                 scale=-1.0, bias=column(half_s, k, j))
+            give(("arg", k, j))
+
+        def product(k, j):
+            r = get("r%d" % j, k)
+            nc.vector.scalar_tensor_tensor(out=r[:], in0=r[:], scalar=column(var, k, j), in1=get("e%d" % j, k)[:],
+                                           op0=ALU.mult, op1=ALU.mult)
+
+        def weigh_t(k):
+            nc.vector.tensor_tensor(out=new("TC", k, [P, P, PACK], F32)[:], in0=at(("T", k))[:].rearrange("p t n -> p n t"),
+                                    in1=get("C", k)[:].rearrange("p h e (o t) -> p (h e o) t", t=PACK), op=ALU.mult)
+            give(("T", k))
+
+        def total_a(k):
+            tc2 = get("TC", k)[:].rearrange("p (h n) t -> p h (n t)", h=2)
+            nc.vector.tensor_tensor(out=new("Z2", k, [P, 2 * P], F32)[:], in0=tc2[:, 0], in1=tc2[:, 1], op=ALU.add)
+
+        def total_b(k):
+            z = get("Z2", k)
+            nc.vector.tensor_tensor(out=new("Z", k, [P, P], F32)[:], in0=z[:, 0:P], in1=z[:, P:], op=ALU.add)
+
+        def invert(k):
+            nc.vector.reciprocal(out=new("rz", k, [P, P], F32)[:], in_=get("Z", k)[:])
+
+        def weigh_q(k):
+            qb = q_sb[:, k % NG, :].unsqueeze(1).broadcast_to([P, OC, PACK])
+            nc.vector.tensor_tensor(out=new("rq", k, [P, OC, PACK], F32)[:], in0=get("rz", k)[:].rearrange("p (o t) -> p o t", t=PACK),
+                                    in1=qb, op=ALU.mult)
+
+        def factor(k):
+            rq = get("rq", k)[:].rearrange("p o t -> p (o t)").unsqueeze(1).broadcast_to([P, NI, P])
+            nc.vector.tensor_tensor(out=new("f", k, [P, NI, P], F32)[:], in0=get("C", k)[:].rearrange("p h e n -> p (h e) n"),
+                                    in1=rq, op=ALU.mult)
+
+        def turn_product(k, j):
+            bank = take(("pt", k, j), [P, PACK, P], F32)
+            for t in range(PACK):
+                nc.tensor.transpose(bank[:, t, :], block(get("r%d" % j, k), t), ident[:])
+
+        def gradient(k, j):
+            gm = new("gm", k, [P, NJ, NI, OC, PACK], BF16, 1, 64) if j == 0 else get("gm", k)
+            nc.vector.tensor_tensor(out=gm[:, j].rearrange("p i o t -> p (i o) t"), in0=at(("pt", k, j))[:].rearrange("p t n -> p n t"),
+                                    in1=get("f", k)[:].rearrange("p i (o t) -> p (i o) t", t=PACK), op=ALU.mult)
+            give(("pt", k, j))
+
+        gq = {}
+
+        def quantise_gm(k):
+            gq[k] = quantise("gq", get("gm", k)[:].rearrange("p j i o t -> p (j i o t)"), 3)
+
+        def out_mm(c, n):
+            bank = take(("out", c, n), [P, KP], F32)
+            for gi in range(NG):
+                mx(bank[:], xuq[gi], n * P, gq[c * NG + gi], 0, KP, gi == 0, gi == NG - 1)
+
+        def out_copy(c, n):
+            res = work.tile([P, NI * NJ, OC], F32, name="res", bufs=4)
+            nc.scalar.activation(out=res[:].rearrange("p (i j) o -> p i j o", i=NI), in_=at(("out", c, n))[:].rearrange("p (j i o) -> p i j o", j=NJ, i=NI), func=ACT.Copy, scale=0.125)
+            give(("out", c, n))
+            dst = out[n * P:(n + 1) * P].rearrange("d i j o -> d (i j) o")[:, :, c * OC:(c + 1) * OC]
+            nc.sync.dma_start(out=dst, in_=res[:])
+
+        nc.vector.tensor_scalar(out=wsn[:], in0=ws[:], scalar1=-1.0, scalar2=None, op0=ALU.mult)
+        widen(False, wide_mu, wb_mu[0][:, 1], ws, 1)
+        widen(True, wide_mu, wb_mu[0][:, 0], ws, 0)
+        widen(False, wide_mu, wb_mu[1][:, 1], ws, 3)
+        turn_x(0, 0)
+        turn_x(0, 1)
+        gain_x(0, 0)
+        widen(True, wide_mu, wb_mu[1][:, 0], ws, 2)
+        gain_x(0, 1)
+        spread_y(0)
+        turn_y(0)
+        variance_columns()
+        copy_y(0)
+        for t in range(2):
+            widen(False, wide_c, wb_c[:, t], ws, t)
+        quantise_xg(0)
+        for j in range(NJ):
+            interleave(True, 0, "mu", j)
+        widen(True, wide_c, wb_c[:, 2], ws, 2)
+        quantise_w(0, "mu")
+        widen(True, wide_c, wb_c[:, 3], ws, 3)
+        for j in range(1, NJ):
+            interleave(True, 0, "c", j)
+        interleave(True, 0, "c", 0)
+        turn_x(1, 0)
+        turn_x(1, 1)
+        for t in range(PACK):
+            widen(False, wide_a, wb_a[:, t], wsn, t)
+        gain_x(1, 0)
+        quantise_w(0, "c")
+        interleave(False, 0, "a", 0)
+        gain_x(1, 1)
+
+        def early(k):
+            c = k // NG + 1
+            if k == 0:
+                quantise_w(0, "a")
+                quantise_xg(1)
+            if c < NC and k % NG == 0:
+                spread_y(c)
+            if c < NC and k % NG == 1:
+                quantise_w(c, "mu")
+                quantise_w(c, "a")
+
+        def next_weights(k, j):
+            c = k // NG + 1
+            if c < NC:
+                interleave(c == 1, c, ("mu", "c")[k % NG], j)
+
+        def next_rest(k):
+            c = k // NG + 1
+            if c < NC and k % NG == 0:
+                interleave(c == 1, c, "a", 0)
+                turn_y(c)
+                copy_y(c)
+            if k < NG:
+                weigh_x(k)
+
+        def late(k):
+            c = k // NG + 1
+            if c < NC and k % NG == 1:
+                quantise_w(c, "c")
+            if 1 <= k <= NG:
+                quantise_xu(k - 1)
+
+        def when(k, step, *args):
+            if 0 <= k < UNITS:
+                step(k, *args)
+
+        def sum_t(k):
+            sum_j("T", "e", k)
+
+        def sum_s(k):
+            sum_j("S", "eg", k)
+
+        def out_product(k, n):
+            if k % NG == 1:
+                out_mm(k // NG, n)
+
+        def out_store(k, n):
+            if k % NG == 1:
+                out_copy(k // NG, n)
+
+        for k in range(UNITS + 2):
+            a, b, c = k, k - 1, k - 2
+            when(b, a_mm)
+            when(a, mu_mm, 0)
+            when(a, d_mm, 1)
+            when(c, weigh_t)
+            when(b, a_copy)
+            when(b, sum_s)
+            when(b, min_pair, 0)
+            when(c, total_a)
+            when(a, d1_copy)
+            when(b, min_pair, 1)
+            when(c, total_b)
+            when(a, d_mm, 2)
+            when(a, d_mm, 3)
+            when(a, mu_mm, 1)
+            when(b, s_copy)
+            when(b, min_j)
+            when(c, invert)
+            when(b, add_a)
+            when(c, weigh_q)
+            when(b, min_i_a)
+            when(c, turn_product, 0)
+            when(a, next_weights, 0)
+            when(a, next_weights, 1)
+            when(c, factor)
+            when(b, min_i_b)
+            when(a, residual, 0)
+            when(b, shift)
+            when(a, square, 0)
+            when(a, next_weights, 2)
+            when(c, turn_product, 1)
+            when(b, arg_mm, 0)
+            when(c, gradient, 0)
+            when(a, residual, 1)
+            when(b, exp_arg, 0)
+            when(b, arg_mm, 1)
+            when(c, turn_product, 2)
+            when(c, gradient, 1)
+            when(a, max_a)
+            when(a, square, 1)
+            when(b, exp_arg, 1)
+            when(b, arg_mm, 2)
+            when(c, turn_product, 3)
+            when(c, gradient, 2)
+            when(a, max_b)
+            when(b, exp_arg, 2)
+            when(b, arg_mm, 3)
+            when(a, mu_mm, 2)
+            when(c, gradient, 3)
+            when(a, mu_mm, 3)
+            when(a, next_weights, 3)
+            when(b, exp_arg, 3)
+            when(a, residual, 2)
+            when(a, gap_j, 2)
+            when(a, cost_mm, 0)
+            when(a, square, 2)
+            when(a, residual, 3)
+            when(b, sum_t)
+            when(a, gap_j, 3)
+            when(a, cost_copy, 0)
+            when(a, square, 3)
+            when(a, cost_mm, 2)
+            when(a, gap_j, 1)
+            when(c, quantise_gm)
+            when(a, cost_copy, 2)
+            when(a, cost_mm, 1)
+            when(a, cost_mm, 3)
+            when(b, product, 0)
+            when(a, cost_copy, 1)
+            when(b, product, 1)
+            when(a, cost_copy, 3)
+            when(a, early)
+            when(a, exp_gap, 0)
+            when(a, exp_gap, 1)
+            when(a, exp_gap, 2)
+            when(a, exp_gap, 3)
+            when(c, out_product, 0)
+            when(c, out_product, 1)
+            when(b, product, 2)
+            when(b, pair)
+            when(b, product, 3)
+            when(b, cofactor)
+            when(c, out_store, 0)
+            when(c, out_store, 1)
+            when(c, out_product, 2)
+            when(c, out_product, 3)
+            when(a, next_rest)
+            when(c, out_store, 2)
+            when(c, out_store, 3)
+            when(a, late)

@@ -72,8 +72,11 @@ def tile_hierarchicalmixtureeffectiveweightgradie_kernel(tc, x, g, w_bytes, w_sc
         wb_a = keep.tile([P, PACK, NI * O], U8, name="wb_a")
         nc.sync.dma_start(out=wb_a[:], in_=wrows[:, :, 32:36, :].rearrange("p t m o -> p t (m o)"))
         nc.sync.dma_start(out=x_sb[1][:], in_=xrows[1])
-        q_sb = keep.tile([P, NG, PACK], BF16, name="q_sb")
-        nc.sync.dma_start(out=q_sb[:], in_=q.rearrange("(g p t) -> p g t", p=P, t=PACK))
+        q_rows = keep.tile([P, 2, P], BF16, name="q_rows")
+        nc.gpsimd.memset(q_rows[:], 0.0)
+        for h in range(2):
+            nc.sync.dma_start(out=q_rows[0:4, h, :].rearrange("r (p e) -> r p e", e=2),
+                              in_=q.rearrange("(r p h e) -> h r p e", p=P // 2, h=2, e=2)[h])
         u_sb = keep.tile([P, NG, PACK], BF16, name="u_sb")
         nc.sync.dma_start(out=u_sb[:], in_=u.rearrange("(g p t) -> p g t", p=P, t=PACK))
 
@@ -143,25 +146,41 @@ def tile_hierarchicalmixtureeffectiveweightgradie_kernel(tc, x, g, w_bytes, w_sc
                 for h in range(2):
                     nc.tensor.transpose(bank[:, tl, h, :], words[:, 2 * half + tl, h::2], ident[:])
 
-        def gain_x(gi, half):
+        def copy_x(gi, half):
             if gi not in xg:
-                xg[gi] = work.tile([P, PACK, P, 2, 2], BF16, name="xgrp", bufs=2, align_bytes=64)
-            bank = at(("xt", gi, half))
-            gb = g4[:].rearrange("p (h e) -> p h e", h=2).unsqueeze(1).broadcast_to([P, P, 2, 2])
-            for tl in range(2):
-                src = bank[:, tl].rearrange("p h n -> p (h n)").bitcast(BF16).rearrange("p (h n e) -> p n h e", h=2, e=2)
-                nc.vector.tensor_tensor(out=xg[gi][:, 2 * half + tl], in0=src, in1=gb, op=ALU.mult)
+                xg[gi] = work.tile([P, 2, P, PACK], F32, name="xt")
+            nc.scalar.copy(out=xg[gi][:, half], in_=at(("xt", gi, half))[:].rearrange("p e h n -> p n (e h)"))
             give(("xt", gi, half))
 
+        xgg = {}
+
+        def gain_x(gi):
+            xgg[gi] = work.tile([P, KP, PACK], BF16, name="xgrp", bufs=2, align_bytes=64)
+            src = xg[gi][:].rearrange("p h n w -> p (h n w)").bitcast(BF16).rearrange("p (n t) -> p n t", t=PACK)
+            nc.vector.tensor_tensor(out=xgg[gi][:], in0=src, in1=g4[:].unsqueeze(1).broadcast_to([P, KP, PACK]), op=ALU.mult)
+
         def quantise_xg(gi):
-            xq[gi] = quantise("xq", xg[gi][:].rearrange("p t n h e -> p (t n h e)"), NG)
+            xq[gi] = quantise("xq", xgg[gi][:].rearrange("p n t -> p (n t)"), NG)
 
         xu = {}
 
+        xw = {}
+
         def weigh_x(gi):
-            xu[gi] = work.tile([P, D, PACK], BF16, name="xgrp", bufs=2, align_bytes=64)
-            ub = u_sb[:, gi, :].unsqueeze(1).broadcast_to([P, D, PACK])
-            nc.vector.tensor_tensor(out=xu[gi][:], in0=x_sb[gi][:].rearrange("p t d -> p d t"), in1=ub, op=ALU.mult)
+            xw[gi] = work.tile([P, PACK, D], BF16, name="xt")
+            for t in range(PACK):
+                nc.vector.tensor_scalar(out=xw[gi][:, t], in0=x_sb[gi][:, t], scalar1=u_sb[:, gi, t:t + 1], scalar2=None, op0=ALU.mult)
+
+        def interleave_x(on_vector, gi, n):
+            if n == 0:
+                xu[gi] = work.tile([P, D, PACK], BF16, name="xgrp", bufs=2, align_bytes=64)
+            cols = slice(n * P, (n + 1) * P)
+            dst = xu[gi][:, cols].rearrange("p (a b) t -> p a t b", b=4)
+            src = xw[gi][:, :, cols].rearrange("p t (a b) -> p a t b", b=4)
+            if on_vector:
+                nc.vector.tensor_copy(out=dst, in_=src)
+            else:
+                nc.scalar.copy(out=dst, in_=src)
 
         def quantise_xu(gi):
             xuq[gi] = quantise("xuq", xu[gi][:].rearrange("p d t -> p (d t)"), NG)
@@ -181,7 +200,8 @@ def tile_hierarchicalmixtureeffectiveweightgradie_kernel(tc, x, g, w_bytes, w_sc
 
         def copy_y(c):
             yt[c] = work.tile([P, NG, KP], BF16, name="yt", bufs=2)
-            nc.scalar.copy(out=yt[c][:].rearrange("p g n -> p (g n)"), in_=at(("yt", c))[:].rearrange("p n m -> p (n m)"))
+            nc.scalar.copy(out=yt[c][:].rearrange("q g (h p e) -> q (g h) p e", h=2, e=2),
+                           in_=at(("yt", c))[:].rearrange("q (m e) p -> q m p e", e=2))
             give(("yt", c))
 
         var = keep.tile([P, NJ * NC], F32, name="var")
@@ -197,6 +217,15 @@ def tile_hierarchicalmixtureeffectiveweightgradie_kernel(tc, x, g, w_bytes, w_sc
             nc.scalar.activation(out=half_s[:], in_=bank[:, 0:NJ * NC], func=ACT.Copy, scale=-0.5)
             nc.scalar.activation(out=half_root[:], in_=root[:], func=ACT.Copy, scale=math.sqrt(0.5))
             give("st")
+
+        q_col = keep.tile([P, NG, 2, 2], F32, name="q_col")
+
+        def q_columns():
+            bank = take("qt", [P, 2, P], BF16)
+            for h in range(2):
+                nc.tensor.transpose(bank[:, h, :], q_rows[:, h, :], ident_bf[:])
+            nc.scalar.copy(out=q_col[:], in_=bank[:, :, 0:4].rearrange("r h (g b) -> r g h b", b=2))
+            give("qt")
 
         def column(tile, k, j):
             n = j * NC + k // NG
@@ -238,47 +267,52 @@ def tile_hierarchicalmixtureeffectiveweightgradie_kernel(tc, x, g, w_bytes, w_sc
 
         def d1_copy(k):
             nc.scalar.copy(out=new("d1", k, [P, KP], F32)[:], in_=at(("d", k, 1))[:])
-            give(("d", k, 1))
 
         def max_a(k):
             nc.vector.scalar_tensor_tensor(out=new("m12", k, [P, KP], F32)[:], in0=at(("d", k, 2))[:], scalar=0.0,
                                            in1=get("d1", k)[:], op0=ALU.max, op1=ALU.max)
 
         def max_b(k):
-            nc.vector.tensor_tensor(out=new("gap0", k, [P, KP], F32)[:], in0=at(("d", k, 3))[:], in1=get("m12", k)[:], op=ALU.max)
+            nc.vector.tensor_tensor(out=new("gap", k, [P, NJ, KP], F32)[:, 0], in0=at(("d", k, 3))[:], in1=get("m12", k)[:], op=ALU.max)
 
         def gap_j(k, j):
-            src = get("d1", k) if j == 1 else at(("d", k, j))
-            nc.vector.tensor_tensor(out=new("gap%d" % j, k, [P, KP], F32)[:], in0=get("gap0", k)[:], in1=src[:], op=ALU.subtract)
-            if j != 1:
-                give(("d", k, j))
+            nc.vector.tensor_tensor(out=get("gap", k)[:, j], in0=get("gap", k)[:, 0], in1=at(("d", k, j))[:], op=ALU.subtract)
+            give(("d", k, j))
 
-        def exp_gap(k, j):
-            eg = new("eg%d" % j, k, [P, KP], F32)
-            nc.scalar.activation(out=eg[:], in_=get("gap%d" % j, k)[:], func=ACT.Exp, scale=-1.0)
+        def exp_gap(k):
+            nc.scalar.activation(out=new("eg", k, [P, NJ, KP], F32)[:], in_=get("gap", k)[:], func=ACT.Exp, scale=-1.0)
 
-        def sum_j(key, name, k):
+        def sum_j(key, k, parts):
             bank = take((key, k), [P, PACK, P], F32)
             for t in range(PACK):
-                turn_sum(bank[:, t, :], [block(get(name + "%d" % j, k), t) for j in range(NJ)])
+                turn_sum(bank[:, t, :], [block(part, t) for part in parts])
+
+        def sum_s(k):
+            sum_j("S", k, [get("eg", k)[:, j] for j in range(NJ)])
+
+        def sum_t(k):
+            sum_j("T", k, [get("e%d" % j, k) for j in range(NJ)])
+
+        def by_gate(ap):
+            return ap.rearrange("p t (i o) -> p i t o", i=NI)
 
         def s_copy(k):
-            nc.scalar.copy(out=new("S", k, [P, P, PACK], F32)[:], in_=at(("S", k))[:].rearrange("p t n -> p n t"))
+            nc.scalar.copy(out=new("S", k, [P, NI, PACK, OC], F32)[:], in_=by_gate(at(("S", k))[:]))
             give(("S", k))
 
         def pair(k):
-            sv = get("S", k)[:].rearrange("p (h e o) t -> p h e (o t)", h=2, e=2)
-            nc.vector.tensor_tensor(out=new("pair", k, [P, 2, P], F32)[:], in0=sv[:, :, 0], in1=sv[:, :, 1], op=ALU.mult)
+            sv = get("S", k)[:].rearrange("p (h e) t o -> p h e (t o)", h=2)
+            nc.gpsimd.tensor_tensor(out=new("pair", k, [P, 2, P], F32)[:], in0=sv[:, :, 0], in1=sv[:, :, 1], op=ALU.mult)
 
         def cofactor(k):
-            sv = get("S", k)[:].rearrange("p (h e o) t -> p h e (o t)", h=2, e=2)
+            sv = get("S", k)[:].rearrange("p (h e) t o -> p h e (t o)", h=2)
             other = get("pair", k)[:, ::-1, :].unsqueeze(2).broadcast_to([P, 2, 2, P])
-            nc.vector.tensor_tensor(out=new("C", k, [P, 2, 2, P], F32, 2)[:], in0=sv[:, :, ::-1, :], in1=other, op=ALU.mult)
+            nc.gpsimd.tensor_tensor(out=new("C", k, [P, 2, 2, P], F32, 2)[:], in0=sv[:, :, ::-1, :], in1=other, op=ALU.mult)
 
         def cost_mm(k, j):
             bank = take(("kn", k, j), [P, PACK, P], F32)
             for t in range(PACK):
-                turn_sum(bank[:, t, :], [block(get("gap%d" % j, k), t), block(get("z2%d" % j, k), t)])
+                turn_sum(bank[:, t, :], [block(get("gap", k)[:, j], t), block(get("z2%d" % j, k), t)])
 
         def cost_copy(k, j):
             kn = new("kn%d" % j, k, [P, KP], F32)
@@ -290,10 +324,6 @@ def tile_hierarchicalmixtureeffectiveweightgradie_kernel(tc, x, g, w_bytes, w_sc
             for t in range(PACK):
                 mx(bank[:, t, :], xq[k % NG], t * P, wq[(k // NG, "a")], 0, P, True, True)
 
-        def a_copy(k):
-            nc.scalar.copy(out=new("na", k, [P, KP], F32)[:], in_=at(("a", k))[:].rearrange("p t n -> p (t n)"))
-            give(("a", k))
-
         def min_pair(k, h):
             n2 = new("n2", k, [P, 2, KP], F32) if h == 0 else get("n2", k)
             nc.vector.tensor_tensor(out=n2[:, h], in0=get("kn%d" % h, k)[:], in1=get("kn%d" % (h + 2), k)[:], op=ALU.min)
@@ -303,7 +333,7 @@ def tile_hierarchicalmixtureeffectiveweightgradie_kernel(tc, x, g, w_bytes, w_sc
             nc.vector.tensor_tensor(out=new("n", k, [P, KP], F32)[:], in0=n2[:, 0], in1=n2[:, 1], op=ALU.min)
 
         def add_a(k):
-            nc.vector.tensor_tensor(out=new("b", k, [P, KP], F32)[:], in0=get("n", k)[:], in1=get("na", k)[:], op=ALU.add)
+            nc.vector.tensor_tensor(out=new("b", k, [P, KP], F32)[:], in0=get("n", k)[:], in1=at(("a", k))[:].rearrange("p t n -> p (t n)"), op=ALU.add)
 
         def min_i_a(k):
             b = get("b", k)[:].rearrange("p (t h n) -> p t h n", t=PACK, h=2)
@@ -317,7 +347,8 @@ def tile_hierarchicalmixtureeffectiveweightgradie_kernel(tc, x, g, w_bytes, w_sc
             low = get("low", k)[:].unsqueeze(2).broadcast_to([P, PACK, NI, OC])
             sh = new("sh", k, [P, KP], F32)
             nc.vector.tensor_tensor(out=sh[:].rearrange("p (t i o) -> p t i o", t=PACK, i=NI),
-                                    in0=get("na", k)[:].rearrange("p (t i o) -> p t i o", t=PACK, i=NI), in1=low, op=ALU.subtract)
+                                    in0=at(("a", k))[:].rearrange("p t (i o) -> p t i o", i=NI), in1=low, op=ALU.subtract)
+            give(("a", k))
 
         def arg_mm(k, j):
             bank = take(("arg", k, j), [P, PACK, P], F32)
@@ -332,16 +363,16 @@ def tile_hierarchicalmixtureeffectiveweightgradie_kernel(tc, x, g, w_bytes, w_sc
 
         def product(k, j):
             r = get("r%d" % j, k)
-            nc.vector.scalar_tensor_tensor(out=r[:], in0=r[:], scalar=column(var, k, j), in1=get("e%d" % j, k)[:],
-                                           op0=ALU.mult, op1=ALU.mult)
+            engine = nc.gpsimd if k < UNITS - 1 else nc.vector
+            engine.tensor_tensor(out=r[:], in0=r[:], in1=get("e%d" % j, k)[:], op=ALU.mult)
 
         def weigh_t(k):
-            nc.vector.tensor_tensor(out=new("TC", k, [P, P, PACK], F32)[:], in0=at(("T", k))[:].rearrange("p t n -> p n t"),
-                                    in1=get("C", k)[:].rearrange("p h e (o t) -> p (h e o) t", t=PACK), op=ALU.mult)
+            nc.vector.tensor_tensor(out=new("TC", k, [P, NI, PACK, OC], F32)[:], in0=by_gate(at(("T", k))[:]),
+                                    in1=get("C", k)[:].rearrange("p h e (t o) -> p (h e) t o", t=PACK), op=ALU.mult)
             give(("T", k))
 
         def total_a(k):
-            tc2 = get("TC", k)[:].rearrange("p (h n) t -> p h (n t)", h=2)
+            tc2 = get("TC", k)[:].rearrange("p (h e) t o -> p h (e t o)", h=2)
             nc.vector.tensor_tensor(out=new("Z2", k, [P, 2 * P], F32)[:], in0=tc2[:, 0], in1=tc2[:, 1], op=ALU.add)
 
         def total_b(k):
@@ -352,75 +383,95 @@ def tile_hierarchicalmixtureeffectiveweightgradie_kernel(tc, x, g, w_bytes, w_sc
             nc.vector.reciprocal(out=new("rz", k, [P, P], F32)[:], in_=get("Z", k)[:])
 
         def weigh_q(k):
-            qb = q_sb[:, k % NG, :].unsqueeze(1).broadcast_to([P, OC, PACK])
-            nc.vector.tensor_tensor(out=new("rq", k, [P, OC, PACK], F32)[:], in0=get("rz", k)[:].rearrange("p (o t) -> p o t", t=PACK),
+            qb = q_col[:, k % NG].rearrange("p h b -> p (h b)").unsqueeze(2).broadcast_to([P, PACK, OC])
+            nc.vector.tensor_tensor(out=new("rq", k, [P, PACK, OC], F32)[:], in0=get("rz", k)[:].rearrange("p (t o) -> p t o", t=PACK),
                                     in1=qb, op=ALU.mult)
 
         def factor(k):
-            rq = get("rq", k)[:].rearrange("p o t -> p (o t)").unsqueeze(1).broadcast_to([P, NI, P])
-            nc.vector.tensor_tensor(out=new("f", k, [P, NI, P], F32)[:], in0=get("C", k)[:].rearrange("p h e n -> p (h e) n"),
-                                    in1=rq, op=ALU.mult)
+            rq = get("rq", k)[:].unsqueeze(1).broadcast_to([P, NI, PACK, OC])
+            nc.vector.tensor_tensor(out=by_gate(new("f", k, [P, PACK, P], F32)[:]),
+                                    in0=get("C", k)[:].rearrange("p h e (t o) -> p (h e) t o", t=PACK), in1=rq, op=ALU.mult)
 
-        def turn_product(k, j):
-            bank = take(("pt", k, j), [P, PACK, P], F32)
+        def turn_factor(k):
+            bank = take(("ft", k), [P, PACK, P], F32)
             for t in range(PACK):
-                nc.tensor.transpose(bank[:, t, :], block(get("r%d" % j, k), t), ident[:])
+                nc.tensor.transpose(bank[:, t, :], get("f", k)[:, t, :], ident[:])
 
         def gradient(k, j):
-            gm = new("gm", k, [P, NJ, NI, OC, PACK], BF16, 1, 64) if j == 0 else get("gm", k)
-            nc.vector.tensor_tensor(out=gm[:, j].rearrange("p i o t -> p (i o) t"), in0=at(("pt", k, j))[:].rearrange("p t n -> p n t"),
-                                    in1=get("f", k)[:].rearrange("p i (o t) -> p (i o) t", t=PACK), op=ALU.mult)
-            give(("pt", k, j))
+            nc.vector.scalar_tensor_tensor(out=new("gm%d" % j, k, [P, KP], BF16)[:], in0=get("r%d" % j, k)[:], scalar=column(var, k, j),
+                                           in1=at(("ft", k))[:].rearrange("p t n -> p (t n)"), op0=ALU.mult, op1=ALU.mult)
+            if j == NJ - 1:
+                give(("ft", k))
+
+        def turn_gradient(k, half):
+            bank = take(("gt", k, half), [P, 2, 2, P], F32)
+            for jj in range(2):
+                words = get("gm%d" % (2 * half + jj), k)[:].bitcast(F32)
+                for h in range(2):
+                    nc.tensor.transpose(bank[:, jj, h, :], block(words, h), ident[:])
+
+        def copy_gradient(k, half):
+            gt = new("gt", k, [P, 2, 2, P, 2], F32, 1, 64) if half == 0 else get("gt", k)
+            nc.scalar.copy(out=gt[:, half], in_=at(("gt", k, half))[:].rearrange("p j h n -> p j n h"))
+            give(("gt", k, half))
 
         gq = {}
 
         def quantise_gm(k):
-            gq[k] = quantise("gq", get("gm", k)[:].rearrange("p j i o t -> p (j i o t)"), 3)
+            gq[k] = quantise("gq", get("gt", k)[:].rearrange("p a j n h -> p (a j n h)").bitcast(BF16), 3)
 
-        def out_mm(c, n):
-            bank = take(("out", c, n), [P, KP], F32)
-            for gi in range(NG):
-                mx(bank[:], xuq[gi], n * P, gq[c * NG + gi], 0, KP, gi == 0, gi == NG - 1)
+        def out_pass(c, n, gi):
+            bank = take(("out", c, n), [P, KP], F32) if gi == 0 else at(("out", c, n))
+            mx(bank[:], xuq[gi], n * P, gq[c * NG + gi], 0, KP, gi == 0, gi == NG - 1)
 
-        def out_copy(c, n):
+        def out_copy(c, n, on_vector):
             res = work.tile([P, NI * NJ, OC], F32, name="res", bufs=4)
-            nc.scalar.activation(out=res[:].rearrange("p (i j) o -> p i j o", i=NI), in_=at(("out", c, n))[:].rearrange("p (j i o) -> p i j o", j=NJ, i=NI), func=ACT.Copy, scale=0.125)
+            dst = res[:].rearrange("p (i j) o -> p i j o", i=NI)
+            src = at(("out", c, n))[:].rearrange("p (j i o) -> p i j o", j=NJ, i=NI)
+            if on_vector:
+                nc.vector.tensor_scalar(out=dst, in0=src, scalar1=0.125, scalar2=None, op0=ALU.mult)
+            else:
+                nc.scalar.activation(out=dst, in_=src, func=ACT.Copy, scale=0.125)
             give(("out", c, n))
             dst = out[n * P:(n + 1) * P].rearrange("d i j o -> d (i j) o")[:, :, c * OC:(c + 1) * OC]
-            nc.sync.dma_start(out=dst, in_=res[:])
+            queue = nc.scalar if on_vector else nc.sync
+            queue.dma_start(out=dst, in_=res[:])
 
         nc.vector.tensor_scalar(out=wsn[:], in0=ws[:], scalar1=-1.0, scalar2=None, op0=ALU.mult)
         widen(False, wide_mu, wb_mu[0][:, 1], ws, 1)
         widen(True, wide_mu, wb_mu[0][:, 0], ws, 0)
-        widen(False, wide_mu, wb_mu[1][:, 1], ws, 3)
         turn_x(0, 0)
         turn_x(0, 1)
-        gain_x(0, 0)
+        copy_x(0, 0)
+        copy_x(0, 1)
         widen(True, wide_mu, wb_mu[1][:, 0], ws, 2)
-        gain_x(0, 1)
+        widen(False, wide_mu, wb_mu[1][:, 1], ws, 3)
         spread_y(0)
-        turn_y(0)
+        gain_x(0)
         variance_columns()
+        turn_y(0)
+        widen(False, wide_c, wb_c[:, 0], ws, 0)
         copy_y(0)
-        for t in range(2):
-            widen(False, wide_c, wb_c[:, t], ws, t)
-        quantise_xg(0)
         for j in range(NJ):
             interleave(True, 0, "mu", j)
-        widen(True, wide_c, wb_c[:, 2], ws, 2)
+        quantise_xg(0)
+        widen(True, wide_c, wb_c[:, 1], ws, 1)
         quantise_w(0, "mu")
+        widen(True, wide_c, wb_c[:, 2], ws, 2)
         widen(True, wide_c, wb_c[:, 3], ws, 3)
+        turn_x(1, 0)
+        turn_x(1, 1)
+        copy_x(1, 0)
+        copy_x(1, 1)
+        for t in range(PACK):
+            widen(False, wide_a, wb_a[:, t], wsn, t)
         for j in range(1, NJ):
             interleave(True, 0, "c", j)
         interleave(True, 0, "c", 0)
-        turn_x(1, 0)
-        turn_x(1, 1)
-        for t in range(PACK):
-            widen(False, wide_a, wb_a[:, t], wsn, t)
-        gain_x(1, 0)
+        gain_x(1)
         quantise_w(0, "c")
         interleave(False, 0, "a", 0)
-        gain_x(1, 1)
+        weigh_x(0)
 
         def early(k):
             c = k // NG + 1
@@ -436,130 +487,138 @@ def tile_hierarchicalmixtureeffectiveweightgradie_kernel(tc, x, g, w_bytes, w_sc
         def next_weights(k, j):
             c = k // NG + 1
             if c < NC:
-                interleave(c == 1, c, ("mu", "c")[k % NG], j)
+                interleave(j == 3 or k < NG, c, ("mu", "c")[k % NG], j)
+            if k < NG:
+                interleave_x(k == 1, k, j)
 
         def next_rest(k):
             c = k // NG + 1
             if c < NC and k % NG == 0:
-                interleave(c == 1, c, "a", 0)
+                interleave(False, c, "a", 0)
                 turn_y(c)
                 copy_y(c)
-            if k < NG:
-                weigh_x(k)
+            if k == 0:
+                q_columns()
 
         def late(k):
             c = k // NG + 1
             if c < NC and k % NG == 1:
                 quantise_w(c, "c")
-            if 1 <= k <= NG:
-                quantise_xu(k - 1)
+            if k < NG:
+                quantise_xu(k)
+            if k == 0:
+                weigh_x(1)
+
+        last = UNITS - 1
 
         def when(k, step, *args):
-            if 0 <= k < UNITS:
+            if 0 <= k <= last:
                 step(k, *args)
 
-        def sum_t(k):
-            sum_j("T", "e", k)
-
-        def sum_s(k):
-            sum_j("S", "eg", k)
-
         def out_product(k, n):
-            if k % NG == 1:
-                out_mm(k // NG, n)
+            if k % NG == 1 and k < last:
+                for gi in range(NG):
+                    out_pass(k // NG, n, gi)
 
         def out_store(k, n):
-            if k % NG == 1:
-                out_copy(k // NG, n)
+            if k % NG == 1 and k < last:
+                out_copy(k // NG, n, False)
+
+        def out_open(k):
+            if k == last:
+                for n in range(D // P):
+                    out_pass(k // NG, n, 0)
 
         for k in range(UNITS + 2):
-            a, b, c = k, k - 1, k - 2
+            a, b, c, d = k, k - 1, k - 2, k - 3
             when(b, a_mm)
-            when(a, mu_mm, 0)
             when(a, d_mm, 1)
+            when(a, d_mm, 2)
             when(c, weigh_t)
-            when(b, a_copy)
             when(b, sum_s)
             when(b, min_pair, 0)
             when(c, total_a)
             when(a, d1_copy)
             when(b, min_pair, 1)
             when(c, total_b)
-            when(a, d_mm, 2)
             when(a, d_mm, 3)
-            when(a, mu_mm, 1)
+            when(d, out_product, 2)
             when(b, s_copy)
+            when(b, pair)
+            when(b, cofactor)
             when(b, min_j)
             when(c, invert)
             when(b, add_a)
             when(c, weigh_q)
             when(b, min_i_a)
-            when(c, turn_product, 0)
+            when(d, out_store, 2)
+            when(d, out_product, 3)
+            when(d, out_store, 3)
+            when(a, mu_mm, 0)
             when(a, next_weights, 0)
             when(a, next_weights, 1)
             when(c, factor)
             when(b, min_i_b)
-            when(a, residual, 0)
+            when(c, turn_factor)
+            when(c, out_open)
+            when(a, max_a)
             when(b, shift)
-            when(a, square, 0)
             when(a, next_weights, 2)
-            when(c, turn_product, 1)
             when(b, arg_mm, 0)
+            when(a, max_b)
             when(c, gradient, 0)
-            when(a, residual, 1)
+            when(a, gap_j, 1)
             when(b, exp_arg, 0)
             when(b, arg_mm, 1)
-            when(c, turn_product, 2)
+            when(a, mu_mm, 1)
+            when(a, residual, 0)
             when(c, gradient, 1)
-            when(a, max_a)
-            when(a, square, 1)
+            when(b, product, 0)
             when(b, exp_arg, 1)
             when(b, arg_mm, 2)
-            when(c, turn_product, 3)
-            when(c, gradient, 2)
-            when(a, max_b)
-            when(b, exp_arg, 2)
-            when(b, arg_mm, 3)
-            when(a, mu_mm, 2)
-            when(c, gradient, 3)
-            when(a, mu_mm, 3)
-            when(a, next_weights, 3)
-            when(b, exp_arg, 3)
-            when(a, residual, 2)
+            when(c, turn_gradient, 0)
+            when(a, square, 0)
             when(a, gap_j, 2)
-            when(a, cost_mm, 0)
-            when(a, square, 2)
-            when(a, residual, 3)
-            when(b, sum_t)
-            when(a, gap_j, 3)
-            when(a, cost_copy, 0)
-            when(a, square, 3)
-            when(a, cost_mm, 2)
-            when(a, gap_j, 1)
-            when(c, quantise_gm)
-            when(a, cost_copy, 2)
-            when(a, cost_mm, 1)
-            when(a, cost_mm, 3)
-            when(b, product, 0)
-            when(a, cost_copy, 1)
+            when(a, residual, 1)
             when(b, product, 1)
+            when(b, exp_arg, 2)
+            when(a, mu_mm, 2)
+            when(b, arg_mm, 3)
+            when(c, gradient, 2)
+            when(a, gap_j, 3)
+            when(a, square, 1)
+            when(b, product, 2)
+            when(b, exp_arg, 3)
+            when(a, mu_mm, 3)
+            when(a, residual, 2)
+            when(c, gradient, 3)
+            when(c, copy_gradient, 0)
+            when(a, cost_mm, 0)
+            when(c, turn_gradient, 1)
+            when(b, product, 3)
+            when(a, residual, 3)
+            when(a, square, 2)
+            when(a, cost_copy, 0)
+            when(b, sum_t)
+            when(c, copy_gradient, 1)
+            when(a, cost_mm, 2)
+            when(a, square, 3)
+            when(a, cost_mm, 1)
+            when(a, cost_copy, 2)
+            when(a, cost_mm, 3)
+            when(a, cost_copy, 1)
             when(a, cost_copy, 3)
+            when(a, next_weights, 3)
             when(a, early)
-            when(a, exp_gap, 0)
-            when(a, exp_gap, 1)
-            when(a, exp_gap, 2)
-            when(a, exp_gap, 3)
+            when(c, quantise_gm)
+            when(a, late)
+            when(a, exp_gap)
             when(c, out_product, 0)
             when(c, out_product, 1)
-            when(b, product, 2)
-            when(b, pair)
-            when(b, product, 3)
-            when(b, cofactor)
             when(c, out_store, 0)
             when(c, out_store, 1)
-            when(c, out_product, 2)
-            when(c, out_product, 3)
             when(a, next_rest)
-            when(c, out_store, 2)
-            when(c, out_store, 3)
-            when(a, late)
+        for n in range(D // P):
+            out_pass(NC - 1, n, NG - 1)
+        for n in range(D // P):
+            out_copy(NC - 1, n, n % 2 == 1)

@@ -240,9 +240,9 @@ def tile_hierarchicalmixtureeffectiveweightgradie_kernel(tc, x, g, w_bytes, w_sc
         def get(name, k):
             return tiles[(name, k)]
 
-        def turn_sum(dst, parts):
+        def turn_sum(dst, parts, plain):
             for n, part in enumerate(parts):
-                nc.tensor.matmul(dst, lhsT=part, rhs=ident[:], start=(n == 0), stop=(n == len(parts) - 1), is_transpose=True)
+                nc.tensor.matmul(dst, lhsT=part, rhs=ident[:], start=(n == 0), stop=(n == len(parts) - 1), is_transpose=not (plain and n == 0))
 
         def block(tile, t):
             return tile[:, t * P:(t + 1) * P]
@@ -252,7 +252,7 @@ def tile_hierarchicalmixtureeffectiveweightgradie_kernel(tc, x, g, w_bytes, w_sc
             mx(bank[:], wq[(k // NG, "mu")], j * P, xq[k % NG], 0, KP, True, True)
 
         def residual(k, j):
-            r = new("r%d" % j, k, [P, KP], F32, 2)
+            r = new("r%d" % j, k, [P, KP], F32, 3)
             nc.vector.tensor_tensor(out=r[:], in0=yt[k // NG][:, k % NG], in1=at(("mu", k, j))[:], op=ALU.subtract)
             give(("mu", k, j))
 
@@ -279,13 +279,15 @@ def tile_hierarchicalmixtureeffectiveweightgradie_kernel(tc, x, g, w_bytes, w_sc
             nc.vector.tensor_tensor(out=get("gap", k)[:, j], in0=get("gap", k)[:, 0], in1=at(("d", k, j))[:], op=ALU.subtract)
             give(("d", k, j))
 
-        def exp_gap(k):
-            nc.scalar.activation(out=new("eg", k, [P, NJ, KP], F32)[:], in_=get("gap", k)[:], func=ACT.Exp, scale=-1.0)
+        def exp_gap(k, half):
+            eg = new("eg", k, [P, NJ, KP], F32) if half == 0 else get("eg", k)
+            rows = slice(2 * half, 2 * half + 2)
+            nc.scalar.activation(out=eg[:, rows], in_=get("gap", k)[:, rows], func=ACT.Exp, scale=-1.0)
 
         def sum_j(key, k, parts):
             bank = take((key, k), [P, PACK, P], F32)
             for t in range(PACK):
-                turn_sum(bank[:, t, :], [block(part, t) for part in parts])
+                turn_sum(bank[:, t, :], [block(part, t) for part in parts], t % 2 == 0)
 
         def sum_s(k):
             sum_j("S", k, [get("eg", k)[:, j] for j in range(NJ)])
@@ -302,7 +304,7 @@ def tile_hierarchicalmixtureeffectiveweightgradie_kernel(tc, x, g, w_bytes, w_sc
 
         def pair(k):
             sv = get("S", k)[:].rearrange("p (h e) t o -> p h e (t o)", h=2)
-            nc.gpsimd.tensor_tensor(out=new("pair", k, [P, 2, P], F32)[:], in0=sv[:, :, 0], in1=sv[:, :, 1], op=ALU.mult)
+            nc.vector.tensor_tensor(out=new("pair", k, [P, 2, P], F32)[:], in0=sv[:, :, 0], in1=sv[:, :, 1], op=ALU.mult)
 
         def cofactor(k):
             sv = get("S", k)[:].rearrange("p (h e) t o -> p h e (t o)", h=2)
@@ -312,7 +314,7 @@ def tile_hierarchicalmixtureeffectiveweightgradie_kernel(tc, x, g, w_bytes, w_sc
         def cost_mm(k, j):
             bank = take(("kn", k, j), [P, PACK, P], F32)
             for t in range(PACK):
-                turn_sum(bank[:, t, :], [block(get("gap", k)[:, j], t), block(get("z2%d" % j, k), t)])
+                turn_sum(bank[:, t, :], [block(get("gap", k)[:, j], t), block(get("z2%d" % j, k), t)], t == 0)
 
         def cost_copy(k, j):
             kn = new("kn%d" % j, k, [P, KP], F32)
@@ -326,17 +328,17 @@ def tile_hierarchicalmixtureeffectiveweightgradie_kernel(tc, x, g, w_bytes, w_sc
 
         def min_pair(k, h):
             n2 = new("n2", k, [P, 2, KP], F32) if h == 0 else get("n2", k)
-            nc.vector.tensor_tensor(out=n2[:, h], in0=get("kn%d" % h, k)[:], in1=get("kn%d" % (h + 2), k)[:], op=ALU.min)
+            nc.vector.tensor_tensor(out=n2[:, h], in0=get("kn%d" % (2 * h), k)[:], in1=get("kn%d" % (2 * h + 1), k)[:], op=ALU.min)
 
         def min_j(k):
             n2 = get("n2", k)
-            nc.vector.tensor_tensor(out=new("n", k, [P, KP], F32)[:], in0=n2[:, 0], in1=n2[:, 1], op=ALU.min)
+            nc.vector.tensor_tensor(out=n2[:, 0], in0=n2[:, 0], in1=n2[:, 1], op=ALU.min)
 
         def add_a(k):
-            nc.vector.tensor_tensor(out=new("b", k, [P, KP], F32)[:], in0=get("n", k)[:], in1=at(("a", k))[:].rearrange("p t n -> p (t n)"), op=ALU.add)
+            nc.vector.tensor_tensor(out=get("n2", k)[:, 1], in0=get("n2", k)[:, 0], in1=at(("a", k))[:].rearrange("p t n -> p (t n)"), op=ALU.add)
 
         def min_i_a(k):
-            b = get("b", k)[:].rearrange("p (t h n) -> p t h n", t=PACK, h=2)
+            b = get("n2", k)[:, 1].rearrange("p (t h n) -> p t h n", t=PACK, h=2)
             nc.vector.tensor_tensor(out=new("b2", k, [P, PACK, 2 * OC], F32)[:], in0=b[:, :, 0], in1=b[:, :, 1], op=ALU.min)
 
         def min_i_b(k):
@@ -353,7 +355,7 @@ def tile_hierarchicalmixtureeffectiveweightgradie_kernel(tc, x, g, w_bytes, w_sc
         def arg_mm(k, j):
             bank = take(("arg", k, j), [P, PACK, P], F32)
             for t in range(PACK):
-                turn_sum(bank[:, t, :], [block(get("kn%d" % j, k), t), block(get("sh", k), t)])
+                turn_sum(bank[:, t, :], [block(get("kn%d" % j, k), t), block(get("sh", k), t)], t == 0 or (k == UNITS - 1 and t == 2))
 
         def exp_arg(k, j):
             e = new("e%d" % j, k, [P, KP], F32)
@@ -363,7 +365,7 @@ def tile_hierarchicalmixtureeffectiveweightgradie_kernel(tc, x, g, w_bytes, w_sc
 
         def product(k, j):
             r = get("r%d" % j, k)
-            engine = nc.gpsimd if k < UNITS - 1 else nc.vector
+            engine = nc.gpsimd if k < UNITS - 1 and j > 0 else nc.vector
             engine.tensor_tensor(out=r[:], in0=r[:], in1=get("e%d" % j, k)[:], op=ALU.mult)
 
         def weigh_t(k):
@@ -437,6 +439,12 @@ def tile_hierarchicalmixtureeffectiveweightgradie_kernel(tc, x, g, w_bytes, w_sc
             queue = nc.scalar if on_vector else nc.sync
             queue.dma_start(out=dst, in_=res[:])
 
+        def weighted_x(gi):
+            weigh_x(gi)
+            for n in range(D // P):
+                interleave_x(True, gi, n)
+            quantise_xu(gi)
+
         nc.vector.tensor_scalar(out=wsn[:], in0=ws[:], scalar1=-1.0, scalar2=None, op0=ALU.mult)
         widen(False, wide_mu, wb_mu[0][:, 1], ws, 1)
         widen(True, wide_mu, wb_mu[0][:, 0], ws, 0)
@@ -445,7 +453,7 @@ def tile_hierarchicalmixtureeffectiveweightgradie_kernel(tc, x, g, w_bytes, w_sc
         copy_x(0, 0)
         copy_x(0, 1)
         widen(True, wide_mu, wb_mu[1][:, 0], ws, 2)
-        widen(False, wide_mu, wb_mu[1][:, 1], ws, 3)
+        widen(True, wide_mu, wb_mu[1][:, 1], ws, 3)
         spread_y(0)
         gain_x(0)
         variance_columns()
@@ -455,7 +463,7 @@ def tile_hierarchicalmixtureeffectiveweightgradie_kernel(tc, x, g, w_bytes, w_sc
         for j in range(NJ):
             interleave(True, 0, "mu", j)
         quantise_xg(0)
-        widen(True, wide_c, wb_c[:, 1], ws, 1)
+        widen(False, wide_c, wb_c[:, 1], ws, 1)
         quantise_w(0, "mu")
         widen(True, wide_c, wb_c[:, 2], ws, 2)
         widen(True, wide_c, wb_c[:, 3], ws, 3)
@@ -471,25 +479,26 @@ def tile_hierarchicalmixtureeffectiveweightgradie_kernel(tc, x, g, w_bytes, w_sc
         gain_x(1)
         quantise_w(0, "c")
         interleave(False, 0, "a", 0)
-        weigh_x(0)
+        quantise_xg(1)
+        weighted_x(0)
+        quantise_w(0, "a")
 
         def early(k):
             c = k // NG + 1
-            if k == 0:
-                quantise_w(0, "a")
-                quantise_xg(1)
+            if c < NC:
+                quantise_w(c, ("c", "mu")[k % NG])
+
+        def early_rest(k):
+            c = k // NG + 1
             if c < NC and k % NG == 0:
                 spread_y(c)
             if c < NC and k % NG == 1:
-                quantise_w(c, "mu")
                 quantise_w(c, "a")
 
         def next_weights(k, j):
             c = k // NG + 1
             if c < NC:
-                interleave(j == 3 or k < NG, c, ("mu", "c")[k % NG], j)
-            if k < NG:
-                interleave_x(k == 1, k, j)
+                interleave(j == 3, c, ("c", "mu")[k % NG], j)
 
         def next_rest(k):
             c = k // NG + 1
@@ -501,13 +510,8 @@ def tile_hierarchicalmixtureeffectiveweightgradie_kernel(tc, x, g, w_bytes, w_sc
                 q_columns()
 
         def late(k):
-            c = k // NG + 1
-            if c < NC and k % NG == 1:
-                quantise_w(c, "c")
-            if k < NG:
-                quantise_xu(k)
             if k == 0:
-                weigh_x(1)
+                weighted_x(1)
 
         last = UNITS - 1
 
@@ -515,109 +519,115 @@ def tile_hierarchicalmixtureeffectiveweightgradie_kernel(tc, x, g, w_bytes, w_sc
             if 0 <= k <= last:
                 step(k, *args)
 
-        def out_product(k, n):
-            if k % NG == 1 and k < last:
-                for gi in range(NG):
-                    out_pass(k // NG, n, gi)
+        def out_rows(k, slot):
+            c, later = divmod(k - 4, NG)
+            if not 0 <= c < NC - 1:
+                return []
+            if c == NC - 2:
+                return [(c, 2 * slot), (c, 2 * slot + 1)] if later == 0 else []
+            return [(c, 2 * later + slot)]
 
-        def out_store(k, n):
-            if k % NG == 1 and k < last:
-                out_copy(k // NG, n, False)
+        def out_product(k, slot):
+            for c, n in out_rows(k, slot):
+                for gi in range(NG):
+                    out_pass(c, n, gi)
+
+        def out_store(k, slot):
+            for c, n in out_rows(k, slot):
+                out_copy(c, n, False)
 
         def out_open(k):
             if k == last:
                 for n in range(D // P):
                     out_pass(k // NG, n, 0)
 
-        for k in range(UNITS + 2):
-            a, b, c, d = k, k - 1, k - 2, k - 3
-            when(b, a_mm)
-            when(a, d_mm, 1)
-            when(a, d_mm, 2)
-            when(c, weigh_t)
-            when(b, sum_s)
-            when(b, min_pair, 0)
-            when(c, total_a)
-            when(a, d1_copy)
-            when(b, min_pair, 1)
-            when(c, total_b)
-            when(a, d_mm, 3)
-            when(d, out_product, 2)
-            when(b, s_copy)
-            when(b, pair)
-            when(b, cofactor)
-            when(b, min_j)
-            when(c, invert)
-            when(b, add_a)
-            when(c, weigh_q)
-            when(b, min_i_a)
-            when(d, out_store, 2)
-            when(d, out_product, 3)
-            when(d, out_store, 3)
-            when(a, mu_mm, 0)
-            when(a, next_weights, 0)
-            when(a, next_weights, 1)
-            when(c, factor)
-            when(b, min_i_b)
-            when(c, turn_factor)
-            when(c, out_open)
-            when(a, max_a)
+        for k in range(-1, UNITS + 2):
+            n, a, b, c = k + 1, k, k - 1, k - 2
             when(b, shift)
-            when(a, next_weights, 2)
             when(b, arg_mm, 0)
+            when(a, residual, 0)
             when(a, max_b)
-            when(c, gradient, 0)
-            when(a, gap_j, 1)
             when(b, exp_arg, 0)
             when(b, arg_mm, 1)
-            when(a, mu_mm, 1)
-            when(a, residual, 0)
-            when(c, gradient, 1)
+            when(a, square, 0)
+            when(a, residual, 1)
+            when(a, gap_j, 1)
             when(b, product, 0)
             when(b, exp_arg, 1)
+            when(a, mu_mm, 2)
+            when(a, mu_mm, 3)
             when(b, arg_mm, 2)
-            when(c, turn_gradient, 0)
-            when(a, square, 0)
+            when(a, square, 1)
+            when(a, residual, 2)
             when(a, gap_j, 2)
-            when(a, residual, 1)
             when(b, product, 1)
             when(b, exp_arg, 2)
-            when(a, mu_mm, 2)
-            when(b, arg_mm, 3)
-            when(c, gradient, 2)
-            when(a, gap_j, 3)
-            when(a, square, 1)
-            when(b, product, 2)
-            when(b, exp_arg, 3)
-            when(a, mu_mm, 3)
-            when(a, residual, 2)
-            when(c, gradient, 3)
-            when(c, copy_gradient, 0)
             when(a, cost_mm, 0)
-            when(c, turn_gradient, 1)
-            when(b, product, 3)
-            when(a, residual, 3)
+            when(b, arg_mm, 3)
             when(a, square, 2)
+            when(a, residual, 3)
+            when(a, gap_j, 3)
+            when(b, product, 2)
             when(a, cost_copy, 0)
-            when(b, sum_t)
-            when(c, copy_gradient, 1)
-            when(a, cost_mm, 2)
-            when(a, square, 3)
+            when(b, exp_arg, 3)
             when(a, cost_mm, 1)
+            when(a, square, 3)
+            when(c, gradient, 0)
+            when(c, gradient, 1)
+            when(b, product, 3)
+            when(a, cost_copy, 1)
+            when(b, sum_t)
+            when(a, exp_gap, 0)
+            when(c, gradient, 2)
+            when(c, gradient, 3)
+            when(a, cost_mm, 2)
+            when(c, turn_gradient, 0)
             when(a, cost_copy, 2)
             when(a, cost_mm, 3)
-            when(a, cost_copy, 1)
-            when(a, cost_copy, 3)
-            when(a, next_weights, 3)
-            when(a, early)
-            when(c, quantise_gm)
+            when(c, copy_gradient, 0)
+            when(c, turn_gradient, 1)
             when(a, late)
-            when(a, exp_gap)
-            when(c, out_product, 0)
-            when(c, out_product, 1)
-            when(c, out_store, 0)
-            when(c, out_store, 1)
+            when(a, min_pair, 0)
+            when(b, weigh_t)
+            when(a, next_weights, 3)
+            when(b, total_a)
+            when(a, early)
+            when(b, total_b)
+            when(a, early_rest)
+            when(a, cost_copy, 3)
+            when(c, copy_gradient, 1)
+            when(a, a_mm)
+            when(n, d_mm, 1)
+            when(a, exp_gap, 1)
+            out_product(k, 0)
+            when(b, invert)
+            when(a, min_pair, 1)
+            when(b, weigh_q)
+            when(a, min_j)
+            when(b, factor)
+            when(a, add_a)
+            when(n, d1_copy)
             when(a, next_rest)
+            when(n, d_mm, 2)
+            when(a, sum_s)
+            out_store(k, 0)
+            when(a, s_copy)
+            out_product(k, 1)
+            when(c, quantise_gm)
+            when(a, min_i_a)
+            when(n, max_a)
+            when(a, min_i_b)
+            when(n, next_weights, 0)
+            when(n, next_weights, 1)
+            when(b, turn_factor)
+            when(b, out_open)
+            when(n, d_mm, 3)
+            out_store(k, 1)
+            when(n, mu_mm, 0)
+            when(n, mu_mm, 1)
+            when(n, next_weights, 2)
+            when(a, pair)
+            when(a, cofactor)
         for n in range(D // P):
             out_pass(NC - 1, n, NG - 1)
         for n in range(D // P):

@@ -19,11 +19,17 @@ ACT = mybir.ActivationFunctionType
 P = 128
 PACK = 4
 KP = P * PACK
-NG = T // KP
+BLOCKS = KP // P
+GROUPS = T // KP
 OC = P // NI
-NC = O // OC
-UNITS = NC * NG
+CHUNKS = O // OC
+UNITS = CHUNKS * GROUPS
+LAST = UNITS - 1
+ROW_TILES = D // P
+EXPERTS = NI * NJ
 BANKS = 8
+RUN = 4
+ON_VECTOR, ON_SCALAR = True, False
 
 
 def tile_hierarchicalmixtureeffectiveweightgradie_kernel(tc, x, g, w_bytes, w_scale, y, s, u, q, out):
@@ -38,10 +44,10 @@ def tile_hierarchicalmixtureeffectiveweightgradie_kernel(tc, x, g, w_bytes, w_sc
         held = {}
 
         def take(key, shape, dtype):
-            b = free_banks[0]
-            free_banks.remove(b)
-            bank = psum.tile(shape, dtype, name="bank%d" % b)
-            held[key] = (b, bank)
+            index = free_banks[0]
+            free_banks.remove(index)
+            bank = psum.tile(shape, dtype, name="bank%d" % index)
+            held[key] = (index, bank)
             return bank
 
         def give(key):
@@ -50,34 +56,39 @@ def tile_hierarchicalmixtureeffectiveweightgradie_kernel(tc, x, g, w_bytes, w_sc
         def at(key):
             return held[key][1]
 
-        wrows = w_bytes.rearrange("(p t) m o -> p t m o", t=PACK)
+        w_rows = w_bytes.rearrange("(p t) m o -> p t m o", t=PACK)
         ws = keep.tile([P, PACK], F32, name="ws")
         nc.sync.dma_start(out=ws[:], in_=w_scale.rearrange("(p t) a b -> p (t a b)", t=PACK))
-        x_sb = [keep.tile([P, PACK, D], BF16, name="x_sb%d" % gi) for gi in range(NG)]
-        xrows = x.rearrange("(g p t) d -> g p t d", p=P, t=PACK)
-        wb_mu = [keep.tile([P, 2, 16 * O], U8, name="wb_mu%d" % h) for h in range(2)]
-        nc.sync.dma_start(out=wb_mu[0][:], in_=wrows[:, 0:2, 0:16, :].rearrange("p t m o -> p t (m o)"))
-        nc.sync.dma_start(out=x_sb[0][:], in_=xrows[0])
-        nc.sync.dma_start(out=wb_mu[1][:], in_=wrows[:, 2:4, 0:16, :].rearrange("p t m o -> p t (m o)"))
         g4 = keep.tile([P, PACK], BF16, name="g4")
         nc.sync.dma_start(out=g4[:], in_=g.rearrange("(p t) -> p t", t=PACK))
-        y_sb = keep.tile([P, NG, PACK, O], BF16, name="y_sb")
+
+        def load_bytes(tile, t0, t1, m0, m1):
+            nc.sync.dma_start(out=tile[:], in_=w_rows[:, t0:t1, m0:m1, :].rearrange("p t m o -> p t (m o)"))
+
+        x_sb = [keep.tile([P, PACK, D], BF16, name="x_sb%d" % group) for group in range(GROUPS)]
+        x_rows = x.rearrange("(g p t) d -> g p t d", p=P, t=PACK)
+        wb_mu = [keep.tile([P, 2, EXPERTS * O], U8, name="wb_mu%d" % part) for part in range(2)]
+        wb_c = [keep.tile([P, 2, EXPERTS * O], U8, name="wb_c%d" % part) for part in range(2)]
+        load_bytes(wb_mu[0], 0, 2, 0, EXPERTS)
+        nc.sync.dma_start(out=x_sb[0][:], in_=x_rows[0])
+        load_bytes(wb_mu[1], 2, 4, 0, EXPERTS)
+        load_bytes(wb_c[0], 0, 2, EXPERTS, 2 * EXPERTS)
+        load_bytes(wb_c[1], 2, 4, EXPERTS, 2 * EXPERTS)
+        y_sb = keep.tile([P, GROUPS, PACK, O], BF16, name="y_sb")
         nc.sync.dma_start(out=y_sb[:], in_=y.rearrange("(g p t) o -> p g t o", p=P, t=PACK))
         s_rows = keep.tile([P, P], BF16, name="s_rows")
         nc.gpsimd.memset(s_rows[:], 0.0)
-        nc.sync.dma_start(out=s_rows[0:16, :].rearrange("r (i o) -> r i o", i=NI),
+        nc.sync.dma_start(out=s_rows[0:NJ * CHUNKS, :].rearrange("r (i o) -> r i o", i=NI),
                           in_=s.rearrange("i j (c o) -> (j c) i o", o=OC))
-        wb_c = keep.tile([P, PACK, 16 * O], U8, name="wb_c")
-        nc.sync.dma_start(out=wb_c[:], in_=wrows[:, :, 16:32, :].rearrange("p t m o -> p t (m o)"))
         wb_a = keep.tile([P, PACK, NI * O], U8, name="wb_a")
-        nc.sync.dma_start(out=wb_a[:], in_=wrows[:, :, 32:36, :].rearrange("p t m o -> p t (m o)"))
-        nc.sync.dma_start(out=x_sb[1][:], in_=xrows[1])
+        load_bytes(wb_a, 0, PACK, 2 * EXPERTS, 2 * EXPERTS + NI)
+        nc.sync.dma_start(out=x_sb[1][:], in_=x_rows[1])
         q_rows = keep.tile([P, 2, P], BF16, name="q_rows")
         nc.gpsimd.memset(q_rows[:], 0.0)
         for h in range(2):
-            nc.sync.dma_start(out=q_rows[0:4, h, :].rearrange("r (p e) -> r p e", e=2),
+            nc.sync.dma_start(out=q_rows[0:2 * GROUPS, h, :].rearrange("r (p e) -> r p e", e=2),
                               in_=q.rearrange("(r p h e) -> h r p e", p=P // 2, h=2, e=2)[h])
-        u_sb = keep.tile([P, NG, PACK], BF16, name="u_sb")
+        u_sb = keep.tile([P, GROUPS, PACK], BF16, name="u_sb")
         nc.sync.dma_start(out=u_sb[:], in_=u.rearrange("(g p t) -> p g t", p=P, t=PACK))
 
         ident = keep.tile([P, P], F32, name="ident")
@@ -86,549 +97,567 @@ def tile_hierarchicalmixtureeffectiveweightgradie_kernel(tc, x, g, w_bytes, w_sc
         make_identity(nc, ident_bf[:])
 
         wsn = keep.tile([P, PACK], F32, name="wsn")
-        wide_mu = keep.tile([P, PACK, NI, NJ, O], BF16, name="wide_mu")
-        wide_c = keep.tile([P, PACK, NI, NJ, O], BF16, name="wide_c")
-        wide_a = keep.tile([P, PACK, NI, 1, O], BF16, name="wide_a")
+        wide = {
+            "mu": keep.tile([P, PACK, NI, NJ, O], BF16, name="wide_mu"),
+            "c": keep.tile([P, PACK, NI, NJ, O], BF16, name="wide_c"),
+            "a": keep.tile([P, PACK, NI, 1, O], BF16, name="wide_a"),
+        }
 
-        def widen(on_vector, wide, wb, scale, t):
-            dst = wide[:, t].rearrange("p i j o -> p (i j o)")
+        def widen(on_vector, kind, codes_in, scale, t):
+            dst = wide[kind][:, t].rearrange("p i j o -> p (i j o)")
             if on_vector:
-                nc.vector.tensor_scalar(out=dst, in0=wb.bitcast(FP8), scalar1=scale[:, t:t + 1], scalar2=None, op0=ALU.mult)
+                nc.vector.tensor_scalar(out=dst, in0=codes_in.bitcast(FP8), scalar1=scale[:, t:t + 1], scalar2=None, op0=ALU.mult)
             else:
-                nc.scalar.activation(out=dst, in_=wb.bitcast(FP8), func=ACT.Copy, scale=scale[:, t:t + 1])
+                nc.scalar.activation(out=dst, in_=codes_in.bitcast(FP8), func=ACT.Copy, scale=scale[:, t:t + 1])
 
         wq = {}
         grouped = {}
-        WIDTH = {"mu": 4, "c": 4, "a": 1}
-        SOURCE = {"mu": wide_mu, "c": wide_c, "a": wide_a}
 
-        def interleave(on_vector, c, kind, j):
-            if (c, kind) not in grouped:
-                grouped[(c, kind)] = work.tile([P, WIDTH[kind], NI, OC, PACK], BF16, name="grp_" + kind, align_bytes=64)
-            src = SOURCE[kind][:, :, :, j, c * OC:(c + 1) * OC]
+        def interleave(on_vector, chunk, kind, j):
+            if (chunk, kind) not in grouped:
+                grouped[(chunk, kind)] = work.tile([P, wide[kind].shape[3], NI, OC, PACK], BF16, name="grp_" + kind, align_bytes=64)
+            src = wide[kind][:, :, :, j, chunk * OC:(chunk + 1) * OC]
+            dst = grouped[(chunk, kind)][:, j]
             if kind == "c" and j == 0:
+                src = src.rearrange("p t i o -> p i o t")
                 if on_vector:
-                    nc.vector.tensor_scalar(out=grouped[(c, kind)][:, j], in0=src.rearrange("p t i o -> p i o t"),
-                                            scalar1=-1.0, scalar2=None, op0=ALU.mult)
+                    nc.vector.tensor_scalar(out=dst, in0=src, scalar1=-1.0, scalar2=None, op0=ALU.mult)
                 else:
-                    nc.scalar.activation(out=grouped[(c, kind)][:, j], in_=src.rearrange("p t i o -> p i o t"),
-                                         func=ACT.Copy, scale=-1.0)
+                    nc.scalar.activation(out=dst, in_=src, func=ACT.Copy, scale=-1.0)
                 return
-            src = src.rearrange("p t i (a b) -> p i a t b", b=4)
-            dst = grouped[(c, kind)][:, j].rearrange("p i (a b) t -> p i a t b", b=4)
+            src = src.rearrange("p t i (a b) -> p i a t b", b=RUN)
+            dst = dst.rearrange("p i (a b) t -> p i a t b", b=RUN)
             if on_vector:
                 nc.vector.tensor_copy(out=dst, in_=src)
             else:
                 nc.scalar.copy(out=dst, in_=src)
 
         def quantise(name, src, bufs):
-            n = src.shape[1] // PACK
-            codes = work.tile([P, n], U32, name=name + "_codes", bufs=bufs, align_bytes=64)
-            scales = work.tile([P, n], U8, name=name + "_scales", bufs=bufs, align_bytes=64)
+            width = src.shape[1] // PACK
+            codes = work.tile([P, width], U32, name=name + "_codes", bufs=bufs, align_bytes=64)
+            scales = work.tile([P, width], U8, name=name + "_scales", bufs=bufs, align_bytes=64)
             nc.vector.quantize_mx(out=codes[:].bitcast(X4), scales=scales[:], in_=src)
             return codes, scales
 
-        def quantise_w(c, kind):
-            wq[(c, kind)] = quantise("wq_" + kind, grouped[(c, kind)][:].rearrange("p j i o t -> p (j i o t)"), 2)
+        def quantise_w(chunk, kind):
+            wq[(chunk, kind)] = quantise("wq_" + kind, grouped[(chunk, kind)][:].rearrange("p j i o t -> p (j i o t)"), 2)
 
-        def mx(dst, lhs, l0, rhs, r0, n, start, stop):
+        def mx(dst, lhs, l0, rhs, r0, width, start, stop):
             nc.tensor.matmul_mx(out=dst, lhsT=lhs[0][:, l0:l0 + P].bitcast(X4), lhsT_scale=lhs[1][:, l0:l0 + P],
-                                rhs=rhs[0][:, r0:r0 + n].bitcast(X4), rhs_scale=rhs[1][:, r0:r0 + n], start=start, stop=stop)
+                                rhs=rhs[0][:, r0:r0 + width].bitcast(X4), rhs_scale=rhs[1][:, r0:r0 + width], start=start, stop=stop)
 
+        x_turned = {}
+        x_gained = {}
         xq = {}
+
+        def turn_x(group, h):
+            words = x_sb[group][:].bitcast(F32)
+            bank = take(("xt", group, h), [P, 2, 2, P], F32)
+            for e in range(2):
+                for w in range(2):
+                    nc.tensor.transpose(bank[:, e, w, :], words[:, 2 * h + e, w::2], ident[:])
+
+        def copy_x(group, h):
+            if group not in x_turned:
+                x_turned[group] = work.tile([P, 2, P, PACK], F32, name="xt")
+            nc.scalar.copy(out=x_turned[group][:, h], in_=at(("xt", group, h))[:].rearrange("d e w p -> d p (e w)"))
+            give(("xt", group, h))
+
+        def gain_x(group):
+            x_gained[group] = work.tile([P, KP, PACK], BF16, name="xgrp", bufs=2, align_bytes=64)
+            src = x_turned[group][:].rearrange("d h p w -> d (h p w)").bitcast(BF16).rearrange("d (col t) -> d col t", t=PACK)
+            nc.vector.tensor_tensor(out=x_gained[group][:], in0=src, in1=g4[:].unsqueeze(1).broadcast_to([P, KP, PACK]), op=ALU.mult)
+
+        def quantise_xg(group):
+            xq[group] = quantise("xq", x_gained[group][:].rearrange("d col t -> d (col t)"), GROUPS)
+
+        x_weighed = {}
         xuq = {}
-        xg = {}
 
-        def turn_x(gi, half):
-            words = x_sb[gi][:].bitcast(F32)
-            bank = take(("xt", gi, half), [P, 2, 2, P], F32)
-            for tl in range(2):
-                for h in range(2):
-                    nc.tensor.transpose(bank[:, tl, h, :], words[:, 2 * half + tl, h::2], ident[:])
-
-        def copy_x(gi, half):
-            if gi not in xg:
-                xg[gi] = work.tile([P, 2, P, PACK], F32, name="xt")
-            nc.scalar.copy(out=xg[gi][:, half], in_=at(("xt", gi, half))[:].rearrange("p e h n -> p n (e h)"))
-            give(("xt", gi, half))
-
-        xgg = {}
-
-        def gain_x(gi):
-            xgg[gi] = work.tile([P, KP, PACK], BF16, name="xgrp", bufs=2, align_bytes=64)
-            src = xg[gi][:].rearrange("p h n w -> p (h n w)").bitcast(BF16).rearrange("p (n t) -> p n t", t=PACK)
-            nc.vector.tensor_tensor(out=xgg[gi][:], in0=src, in1=g4[:].unsqueeze(1).broadcast_to([P, KP, PACK]), op=ALU.mult)
-
-        def quantise_xg(gi):
-            xq[gi] = quantise("xq", xgg[gi][:].rearrange("p n t -> p (n t)"), NG)
-
-        xu = {}
-
-        xw = {}
-
-        def weigh_x(gi):
-            xw[gi] = work.tile([P, PACK, D], BF16, name="xt")
+        def weigh_x(group):
+            rows = work.tile([P, PACK, D], BF16, name="xt")
             for t in range(PACK):
-                nc.vector.tensor_scalar(out=xw[gi][:, t], in0=x_sb[gi][:, t], scalar1=u_sb[:, gi, t:t + 1], scalar2=None, op0=ALU.mult)
+                nc.vector.tensor_scalar(out=rows[:, t], in0=x_sb[group][:, t], scalar1=u_sb[:, group, t:t + 1], scalar2=None, op0=ALU.mult)
+            x_weighed[group] = work.tile([P, D, PACK], BF16, name="xgrp", bufs=2, align_bytes=64)
+            nc.vector.tensor_copy(out=x_weighed[group][:].rearrange("p (a b) t -> p a t b", b=RUN),
+                                  in_=rows[:].rearrange("p t (a b) -> p a t b", b=RUN))
 
-        def interleave_x(on_vector, gi, n):
-            if n == 0:
-                xu[gi] = work.tile([P, D, PACK], BF16, name="xgrp", bufs=2, align_bytes=64)
-            cols = slice(n * P, (n + 1) * P)
-            dst = xu[gi][:, cols].rearrange("p (a b) t -> p a t b", b=4)
-            src = xw[gi][:, :, cols].rearrange("p t (a b) -> p a t b", b=4)
-            if on_vector:
-                nc.vector.tensor_copy(out=dst, in_=src)
-            else:
-                nc.scalar.copy(out=dst, in_=src)
+        def quantise_xu(group):
+            xuq[group] = quantise("xuq", x_weighed[group][:].rearrange("p d t -> p (d t)"), GROUPS)
 
-        def quantise_xu(gi):
-            xuq[gi] = quantise("xuq", xu[gi][:].rearrange("p d t -> p (d t)"), NG)
+        y_spread = {}
+        y_turned = {}
 
-        yt = {}
-        yrep = {}
+        def spread_y(chunk):
+            y_spread[chunk] = work.tile([P, GROUPS * PACK, NI, OC], BF16, name="yrep")
+            src = y_sb[:].rearrange("p g t o -> p (g t) o")[:, :, chunk * OC:(chunk + 1) * OC]
+            nc.vector.tensor_copy(out=y_spread[chunk][:], in_=src.unsqueeze(2).broadcast_to([P, GROUPS * PACK, NI, OC]))
 
-        def spread_y(c):
-            yrep[c] = work.tile([P, NG * PACK, NI, OC], BF16, name="yrep")
-            src = y_sb[:].rearrange("p g t o -> p (g t) o")[:, :, c * OC:(c + 1) * OC].unsqueeze(2).broadcast_to([P, NG * PACK, NI, OC])
-            nc.vector.tensor_copy(out=yrep[c][:], in_=src)
+        def turn_y(chunk):
+            bank = take(("yt", chunk), [P, GROUPS * PACK, P], BF16)
+            for row in range(GROUPS * PACK):
+                nc.tensor.transpose(bank[:, row, :], y_spread[chunk][:, row].rearrange("p i o -> p (i o)"), ident_bf[:])
+            y_turned[chunk] = work.tile([P, GROUPS, KP], BF16, name="yt", bufs=2)
+            nc.scalar.copy(out=y_turned[chunk][:].rearrange("m g (h p e) -> m (g h) p e", h=2, e=2),
+                           in_=bank[:].rearrange("m (gh e) p -> m gh p e", e=2))
+            give(("yt", chunk))
 
-        def turn_y(c):
-            bank = take(("yt", c), [P, NG * PACK, P], BF16)
-            for n in range(NG * PACK):
-                nc.tensor.transpose(bank[:, n, :], yrep[c][:, n].rearrange("p i o -> p (i o)"), ident_bf[:])
-
-        def copy_y(c):
-            yt[c] = work.tile([P, NG, KP], BF16, name="yt", bufs=2)
-            nc.scalar.copy(out=yt[c][:].rearrange("q g (h p e) -> q (g h) p e", h=2, e=2),
-                           in_=at(("yt", c))[:].rearrange("q (m e) p -> q m p e", e=2))
-            give(("yt", c))
-
-        var = keep.tile([P, NJ * NC], F32, name="var")
-        root = keep.tile([P, NJ * NC], F32, name="root")
-        half_root = keep.tile([P, NJ * NC], F32, name="half_root")
-        half_s = keep.tile([P, NJ * NC], F32, name="half_s")
+        var = keep.tile([P, NJ * CHUNKS], F32, name="var")
+        root = keep.tile([P, NJ * CHUNKS], F32, name="root")
+        half_root = keep.tile([P, NJ * CHUNKS], F32, name="half_root")
+        half_s = keep.tile([P, NJ * CHUNKS], F32, name="half_s")
 
         def variance_columns():
             bank = take("st", [P, P], BF16)
             nc.tensor.transpose(bank[:], s_rows[:], ident_bf[:])
-            nc.scalar.activation(out=var[:], in_=bank[:, 0:NJ * NC], func=ACT.Exp, scale=-1.0)
-            nc.scalar.activation(out=root[:], in_=bank[:, 0:NJ * NC], func=ACT.Exp, scale=-0.5)
-            nc.scalar.activation(out=half_s[:], in_=bank[:, 0:NJ * NC], func=ACT.Copy, scale=-0.5)
+            nc.scalar.activation(out=var[:], in_=bank[:, 0:NJ * CHUNKS], func=ACT.Exp, scale=-1.0)
+            nc.scalar.activation(out=root[:], in_=bank[:, 0:NJ * CHUNKS], func=ACT.Exp, scale=-0.5)
+            nc.scalar.activation(out=half_s[:], in_=bank[:, 0:NJ * CHUNKS], func=ACT.Copy, scale=-0.5)
             nc.scalar.activation(out=half_root[:], in_=root[:], func=ACT.Copy, scale=math.sqrt(0.5))
             give("st")
 
-        q_col = keep.tile([P, NG, 2, 2], F32, name="q_col")
+        def column(tile, unit, j):
+            index = j * CHUNKS + unit // GROUPS
+            return tile[:, index:index + 1]
+
+        q_col = keep.tile([P, GROUPS, 2, 2], F32, name="q_col")
 
         def q_columns():
             bank = take("qt", [P, 2, P], BF16)
             for h in range(2):
                 nc.tensor.transpose(bank[:, h, :], q_rows[:, h, :], ident_bf[:])
-            nc.scalar.copy(out=q_col[:], in_=bank[:, :, 0:4].rearrange("r h (g b) -> r g h b", b=2))
+            nc.scalar.copy(out=q_col[:], in_=bank[:, :, 0:2 * GROUPS].rearrange("m h (g b) -> m g h b", b=2))
             give("qt")
-
-        def column(tile, k, j):
-            n = j * NC + k // NG
-            return tile[:, n:n + 1]
 
         tiles = {}
 
-        def new(name, k, shape, dtype, bufs=1, align=32):
-            tiles[(name, k)] = work.tile(shape, dtype, name=name, bufs=bufs, align_bytes=align)
-            return tiles[(name, k)]
+        def new(name, unit, shape, dtype, bufs=1, align=32):
+            tiles[(name, unit)] = work.tile(shape, dtype, name=name, bufs=bufs, align_bytes=align)
+            return tiles[(name, unit)]
 
-        def get(name, k):
-            return tiles[(name, k)]
+        def get(name, unit):
+            return tiles[(name, unit)]
 
-        def turn_sum(dst, parts, plain):
-            for n, part in enumerate(parts):
-                nc.tensor.matmul(dst, lhsT=part, rhs=ident[:], start=(n == 0), stop=(n == len(parts) - 1), is_transpose=not (plain and n == 0))
+        def block(tile, b):
+            return tile[:, b * P:(b + 1) * P]
 
-        def block(tile, t):
-            return tile[:, t * P:(t + 1) * P]
-
-        def mu_mm(k, j):
-            bank = take(("mu", k, j), [P, KP], F32)
-            mx(bank[:], wq[(k // NG, "mu")], j * P, xq[k % NG], 0, KP, True, True)
-
-        def residual(k, j):
-            r = new("r%d" % j, k, [P, KP], F32, 3)
-            nc.vector.tensor_tensor(out=r[:], in0=yt[k // NG][:, k % NG], in1=at(("mu", k, j))[:], op=ALU.subtract)
-            give(("mu", k, j))
-
-        def square(k, j):
-            z2 = new("z2%d" % j, k, [P, KP], F32)
-            nc.scalar.activation(out=z2[:], in_=get("r%d" % j, k)[:], func=ACT.Square, scale=column(half_root, k, j))
-
-        def d_mm(k, j):
-            bank = take(("d", k, j), [P, KP], F32)
-            mx(bank[:], wq[(k // NG, "c")], j * P, xq[k % NG], 0, KP, True, False)
-            mx(bank[:], wq[(k // NG, "c")], 0, xq[k % NG], 0, KP, False, True)
-
-        def d1_copy(k):
-            nc.scalar.copy(out=new("d1", k, [P, KP], F32)[:], in_=at(("d", k, 1))[:])
-
-        def max_a(k):
-            nc.vector.scalar_tensor_tensor(out=new("m12", k, [P, KP], F32)[:], in0=at(("d", k, 2))[:], scalar=0.0,
-                                           in1=get("d1", k)[:], op0=ALU.max, op1=ALU.max)
-
-        def max_b(k):
-            nc.vector.tensor_tensor(out=new("gap", k, [P, NJ, KP], F32)[:, 0], in0=at(("d", k, 3))[:], in1=get("m12", k)[:], op=ALU.max)
-
-        def gap_j(k, j):
-            nc.vector.tensor_tensor(out=get("gap", k)[:, j], in0=get("gap", k)[:, 0], in1=at(("d", k, j))[:], op=ALU.subtract)
-            give(("d", k, j))
-
-        def exp_gap(k, half):
-            eg = new("eg", k, [P, NJ, KP], F32) if half == 0 else get("eg", k)
-            rows = slice(2 * half, 2 * half + 2)
-            nc.scalar.activation(out=eg[:, rows], in_=get("gap", k)[:, rows], func=ACT.Exp, scale=-1.0)
-
-        def sum_j(key, k, parts):
-            bank = take((key, k), [P, PACK, P], F32)
-            for t in range(PACK):
-                turn_sum(bank[:, t, :], [block(part, t) for part in parts], t % 2 == 0)
-
-        def sum_s(k):
-            sum_j("S", k, [get("eg", k)[:, j] for j in range(NJ)])
-
-        def sum_t(k):
-            sum_j("T", k, [get("e%d" % j, k) for j in range(NJ)])
+        def flat(bank):
+            return bank[:].rearrange("p b m -> p (b m)")
 
         def by_gate(ap):
-            return ap.rearrange("p t (i o) -> p i t o", i=NI)
+            return ap.rearrange("p b (i o) -> p i b o", i=NI)
 
-        def s_copy(k):
-            nc.scalar.copy(out=new("S", k, [P, NI, PACK, OC], F32)[:], in_=by_gate(at(("S", k))[:]))
-            give(("S", k))
+        def turn_sum(key, parts, plain_block):
+            bank = take(key, [P, BLOCKS, P], F32)
+            for b in range(BLOCKS):
+                for index, part in enumerate(parts):
+                    nc.tensor.matmul(bank[:, b, :], lhsT=block(part, b), rhs=ident[:], start=(index == 0), stop=(index == len(parts) - 1),
+                                     is_transpose=not (b == plain_block and index == 0))
 
-        def pair(k):
-            sv = get("S", k)[:].rearrange("p (h e) t o -> p h e (t o)", h=2)
-            nc.vector.tensor_tensor(out=new("pair", k, [P, 2, P], F32)[:], in0=sv[:, :, 0], in1=sv[:, :, 1], op=ALU.mult)
+        def mu_mm(unit, j):
+            bank = take(("mu", unit, j), [P, KP], F32)
+            mx(bank[:], wq[(unit // GROUPS, "mu")], j * P, xq[unit % GROUPS], 0, KP, True, True)
 
-        def cofactor(k):
-            sv = get("S", k)[:].rearrange("p (h e) t o -> p h e (t o)", h=2)
-            other = get("pair", k)[:, ::-1, :].unsqueeze(2).broadcast_to([P, 2, 2, P])
-            nc.gpsimd.tensor_tensor(out=new("C", k, [P, 2, 2, P], F32, 2)[:], in0=sv[:, :, ::-1, :], in1=other, op=ALU.mult)
+        def residual(unit, j):
+            r = new("r%d" % j, unit, [P, KP], F32, 3)
+            nc.vector.tensor_tensor(out=r[:], in0=y_turned[unit // GROUPS][:, unit % GROUPS], in1=at(("mu", unit, j))[:], op=ALU.subtract)
+            give(("mu", unit, j))
 
-        def cost_mm(k, j):
-            bank = take(("kn", k, j), [P, PACK, P], F32)
-            for t in range(PACK):
-                turn_sum(bank[:, t, :], [block(get("gap", k)[:, j], t), block(get("z2%d" % j, k), t)], t == 0)
+        def square(unit, j):
+            z2 = new("z2%d" % j, unit, [P, KP], F32)
+            nc.scalar.activation(out=z2[:], in_=get("r%d" % j, unit)[:], func=ACT.Square, scale=column(half_root, unit, j))
 
-        def cost_copy(k, j):
-            kn = new("kn%d" % j, k, [P, KP], F32)
-            nc.scalar.copy(out=kn[:], in_=at(("kn", k, j))[:].rearrange("p t n -> p (t n)"))
-            give(("kn", k, j))
+        def d_mm(unit, j):
+            bank = take(("d", unit, j), [P, KP], F32)
+            mx(bank[:], wq[(unit // GROUPS, "c")], j * P, xq[unit % GROUPS], 0, KP, True, False)
+            mx(bank[:], wq[(unit // GROUPS, "c")], 0, xq[unit % GROUPS], 0, KP, False, True)
 
-        def a_mm(k):
-            bank = take(("a", k), [P, PACK, P], F32)
-            for t in range(PACK):
-                mx(bank[:, t, :], xq[k % NG], t * P, wq[(k // NG, "a")], 0, P, True, True)
+        def d1_copy(unit):
+            nc.scalar.copy(out=new("d1", unit, [P, KP], F32)[:], in_=at(("d", unit, 1))[:])
 
-        def min_pair(k, h):
-            n2 = new("n2", k, [P, 2, KP], F32) if h == 0 else get("n2", k)
-            nc.vector.tensor_tensor(out=n2[:, h], in0=get("kn%d" % (2 * h), k)[:], in1=get("kn%d" % (2 * h + 1), k)[:], op=ALU.min)
+        def max_12(unit):
+            nc.vector.scalar_tensor_tensor(out=new("m12", unit, [P, KP], F32)[:], in0=at(("d", unit, 2))[:], scalar=0.0,
+                                           in1=get("d1", unit)[:], op0=ALU.max, op1=ALU.max)
 
-        def min_j(k):
-            n2 = get("n2", k)
-            nc.vector.tensor_tensor(out=n2[:, 0], in0=n2[:, 0], in1=n2[:, 1], op=ALU.min)
+        def max_123(unit):
+            nc.vector.tensor_tensor(out=new("gap", unit, [P, NJ, KP], F32)[:, 0], in0=at(("d", unit, 3))[:], in1=get("m12", unit)[:], op=ALU.max)
 
-        def add_a(k):
-            nc.vector.tensor_tensor(out=get("n2", k)[:, 1], in0=get("n2", k)[:, 0], in1=at(("a", k))[:].rearrange("p t n -> p (t n)"), op=ALU.add)
+        def gap_j(unit, j):
+            gap = get("gap", unit)
+            nc.vector.tensor_tensor(out=gap[:, j], in0=gap[:, 0], in1=at(("d", unit, j))[:], op=ALU.subtract)
+            give(("d", unit, j))
 
-        def min_i_a(k):
-            b = get("n2", k)[:, 1].rearrange("p (t h n) -> p t h n", t=PACK, h=2)
-            nc.vector.tensor_tensor(out=new("b2", k, [P, PACK, 2 * OC], F32)[:], in0=b[:, :, 0], in1=b[:, :, 1], op=ALU.min)
+        def exp_gap(unit, half):
+            eg = new("eg", unit, [P, NJ, KP], F32) if half == 0 else get("eg", unit)
+            rows = slice(2 * half, 2 * half + 2)
+            nc.scalar.activation(out=eg[:, rows], in_=get("gap", unit)[:, rows], func=ACT.Exp, scale=-1.0)
 
-        def min_i_b(k):
-            b2 = get("b2", k)
-            nc.vector.tensor_tensor(out=new("low", k, [P, PACK, OC], F32)[:], in0=b2[:, :, 0:OC], in1=b2[:, :, OC:], op=ALU.min)
+        def sum_s(unit):
+            turn_sum(("S", unit), [get("eg", unit)[:, j] for j in range(NJ)], 2)
 
-        def shift(k):
-            low = get("low", k)[:].unsqueeze(2).broadcast_to([P, PACK, NI, OC])
-            sh = new("sh", k, [P, KP], F32)
-            nc.vector.tensor_tensor(out=sh[:].rearrange("p (t i o) -> p t i o", t=PACK, i=NI),
-                                    in0=at(("a", k))[:].rearrange("p t (i o) -> p t i o", i=NI), in1=low, op=ALU.subtract)
-            give(("a", k))
+        def s_copy(unit):
+            nc.scalar.copy(out=new("S", unit, [P, NI, BLOCKS, OC], F32)[:], in_=by_gate(at(("S", unit))[:]))
+            give(("S", unit))
 
-        def arg_mm(k, j):
-            bank = take(("arg", k, j), [P, PACK, P], F32)
-            for t in range(PACK):
-                turn_sum(bank[:, t, :], [block(get("kn%d" % j, k), t), block(get("sh", k), t)], t == 0 or (k == UNITS - 1 and t == 2))
+        def s_pairs(unit):
+            return get("S", unit)[:].rearrange("p (i1 i0) b o -> p i1 i0 (b o)", i1=2)
 
-        def exp_arg(k, j):
-            e = new("e%d" % j, k, [P, KP], F32)
-            nc.scalar.activation(out=e[:], in_=at(("arg", k, j))[:].rearrange("p t n -> p (t n)"), func=ACT.Exp,
-                                 scale=-1.0, bias=column(half_s, k, j))
-            give(("arg", k, j))
+        def pair(unit):
+            nc.vector.tensor_tensor(out=new("pair", unit, [P, 2, P], F32)[:], in0=s_pairs(unit)[:, :, 0], in1=s_pairs(unit)[:, :, 1], op=ALU.mult)
 
-        def product(k, j):
-            r = get("r%d" % j, k)
-            engine = nc.gpsimd if k < UNITS - 1 and j > 0 else nc.vector
-            engine.tensor_tensor(out=r[:], in0=r[:], in1=get("e%d" % j, k)[:], op=ALU.mult)
+        def cofactor(unit):
+            other = get("pair", unit)[:, ::-1, :].unsqueeze(2).broadcast_to([P, 2, 2, P])
+            nc.gpsimd.tensor_tensor(out=new("C", unit, [P, 2, 2, P], F32, 2)[:], in0=s_pairs(unit)[:, :, ::-1, :], in1=other, op=ALU.mult)
 
-        def weigh_t(k):
-            nc.vector.tensor_tensor(out=new("TC", k, [P, NI, PACK, OC], F32)[:], in0=by_gate(at(("T", k))[:]),
-                                    in1=get("C", k)[:].rearrange("p h e (t o) -> p (h e) t o", t=PACK), op=ALU.mult)
-            give(("T", k))
+        def cofactors(unit):
+            return get("C", unit)[:].rearrange("p i1 i0 (b o) -> p (i1 i0) b o", b=BLOCKS)
 
-        def total_a(k):
-            tc2 = get("TC", k)[:].rearrange("p (h e) t o -> p h (e t o)", h=2)
-            nc.vector.tensor_tensor(out=new("Z2", k, [P, 2 * P], F32)[:], in0=tc2[:, 0], in1=tc2[:, 1], op=ALU.add)
+        def cost_mm(unit, j):
+            turn_sum(("cost", unit, j), [get("gap", unit)[:, j], get("z2%d" % j, unit)], 0)
 
-        def total_b(k):
-            z = get("Z2", k)
-            nc.vector.tensor_tensor(out=new("Z", k, [P, P], F32)[:], in0=z[:, 0:P], in1=z[:, P:], op=ALU.add)
+        def cost_copy(unit, j):
+            nc.scalar.copy(out=new("cost%d" % j, unit, [P, KP], F32)[:], in_=flat(at(("cost", unit, j))))
+            give(("cost", unit, j))
 
-        def invert(k):
-            nc.vector.reciprocal(out=new("rz", k, [P, P], F32)[:], in_=get("Z", k)[:])
+        def a_mm(unit):
+            bank = take(("a", unit), [P, BLOCKS, P], F32)
+            for b in range(BLOCKS):
+                mx(bank[:, b, :], xq[unit % GROUPS], b * P, wq[(unit // GROUPS, "a")], 0, P, True, True)
 
-        def weigh_q(k):
-            qb = q_col[:, k % NG].rearrange("p h b -> p (h b)").unsqueeze(2).broadcast_to([P, PACK, OC])
-            nc.vector.tensor_tensor(out=new("rq", k, [P, PACK, OC], F32)[:], in0=get("rz", k)[:].rearrange("p (t o) -> p t o", t=PACK),
-                                    in1=qb, op=ALU.mult)
+        def min_pair(unit, half):
+            least = new("least", unit, [P, 2, KP], F32) if half == 0 else get("least", unit)
+            nc.vector.tensor_tensor(out=least[:, half], in0=get("cost%d" % (2 * half), unit)[:], in1=get("cost%d" % (2 * half + 1), unit)[:], op=ALU.min)
 
-        def factor(k):
-            rq = get("rq", k)[:].unsqueeze(1).broadcast_to([P, NI, PACK, OC])
-            nc.vector.tensor_tensor(out=by_gate(new("f", k, [P, PACK, P], F32)[:]),
-                                    in0=get("C", k)[:].rearrange("p h e (t o) -> p (h e) t o", t=PACK), in1=rq, op=ALU.mult)
+        def min_j(unit):
+            least = get("least", unit)
+            nc.vector.tensor_tensor(out=least[:, 0], in0=least[:, 0], in1=least[:, 1], op=ALU.min)
 
-        def turn_factor(k):
-            bank = take(("ft", k), [P, PACK, P], F32)
-            for t in range(PACK):
-                nc.tensor.transpose(bank[:, t, :], get("f", k)[:, t, :], ident[:])
+        def add_a(unit):
+            least = get("least", unit)
+            nc.vector.tensor_tensor(out=least[:, 1], in0=least[:, 0], in1=flat(at(("a", unit))), op=ALU.add)
 
-        def gradient(k, j):
-            nc.vector.scalar_tensor_tensor(out=new("gm%d" % j, k, [P, KP], BF16)[:], in0=get("r%d" % j, k)[:], scalar=column(var, k, j),
-                                           in1=at(("ft", k))[:].rearrange("p t n -> p (t n)"), op0=ALU.mult, op1=ALU.mult)
+        def min_i1(unit):
+            gated = get("least", unit)[:, 1].rearrange("p (b i1 m) -> p b i1 m", b=BLOCKS, i1=2)
+            nc.vector.tensor_tensor(out=new("low2", unit, [P, BLOCKS, 2 * OC], F32)[:], in0=gated[:, :, 0], in1=gated[:, :, 1], op=ALU.min)
+
+        def min_i0(unit):
+            low2 = get("low2", unit)
+            nc.vector.tensor_tensor(out=new("low", unit, [P, BLOCKS, OC], F32)[:], in0=low2[:, :, 0:OC], in1=low2[:, :, OC:], op=ALU.min)
+
+        def shift(unit):
+            low = get("low", unit)[:].unsqueeze(2).broadcast_to([P, BLOCKS, NI, OC])
+            nc.vector.tensor_tensor(out=new("shift", unit, [P, KP], F32)[:].rearrange("p (b i o) -> p b i o", b=BLOCKS, i=NI),
+                                    in0=at(("a", unit))[:].rearrange("p b (i o) -> p b i o", i=NI), in1=low, op=ALU.subtract)
+            give(("a", unit))
+
+        def arg_mm(unit, j):
+            turn_sum(("arg", unit, j), [get("cost%d" % j, unit), get("shift", unit)], None if j == 2 and unit < LAST else 0)
+
+        def exp_arg(unit, j):
+            nc.scalar.activation(out=new("e%d" % j, unit, [P, KP], F32)[:], in_=flat(at(("arg", unit, j))), func=ACT.Exp,
+                                 scale=-1.0, bias=column(half_s, unit, j))
+            give(("arg", unit, j))
+
+        def product(unit, j):
+            r = get("r%d" % j, unit)
+            engine = nc.gpsimd if 0 < unit < LAST and j > 0 else nc.vector
+            engine.tensor_tensor(out=r[:], in0=r[:], in1=get("e%d" % j, unit)[:], op=ALU.mult)
+
+        def sum_e(unit):
+            turn_sum(("E", unit), [get("e%d" % j, unit) for j in range(NJ)], 2)
+
+        def weigh_sums(unit):
+            nc.vector.tensor_tensor(out=new("EC", unit, [P, NI, BLOCKS, OC], F32)[:], in0=by_gate(at(("E", unit))[:]),
+                                    in1=cofactors(unit), op=ALU.mult)
+            give(("E", unit))
+
+        def total_i1(unit):
+            terms = get("EC", unit)[:].rearrange("p (i1 i0) b o -> p i1 (i0 b o)", i1=2)
+            nc.vector.tensor_tensor(out=new("Z2", unit, [P, 2 * P], F32)[:], in0=terms[:, 0], in1=terms[:, 1], op=ALU.add)
+
+        def total_i0(unit):
+            z_two = get("Z2", unit)
+            nc.vector.tensor_tensor(out=new("Z", unit, [P, P], F32)[:], in0=z_two[:, 0:P], in1=z_two[:, P:], op=ALU.add)
+
+        def invert(unit):
+            nc.vector.reciprocal(out=new("rz", unit, [P, P], F32)[:], in_=get("Z", unit)[:])
+
+        def weigh_q(unit):
+            q_spread = q_col[:, unit % GROUPS].rearrange("p h b -> p (h b)").unsqueeze(2).broadcast_to([P, BLOCKS, OC])
+            nc.vector.tensor_tensor(out=new("rq", unit, [P, BLOCKS, OC], F32)[:], in0=get("rz", unit)[:].rearrange("p (b o) -> p b o", b=BLOCKS),
+                                    in1=q_spread, op=ALU.mult)
+
+        def factor(unit):
+            rq = get("rq", unit)[:].unsqueeze(1).broadcast_to([P, NI, BLOCKS, OC])
+            nc.vector.tensor_tensor(out=by_gate(new("f", unit, [P, BLOCKS, P], F32)[:]), in0=cofactors(unit), in1=rq, op=ALU.mult)
+
+        def turn_factor(unit):
+            bank = take(("ft", unit), [P, BLOCKS, P], F32)
+            for b in range(BLOCKS):
+                nc.tensor.transpose(bank[:, b, :], get("f", unit)[:, b, :], ident[:])
+
+        def gradient(unit, j):
+            nc.vector.scalar_tensor_tensor(out=new("gm%d" % j, unit, [P, KP], BF16)[:], in0=get("r%d" % j, unit)[:], scalar=column(var, unit, j),
+                                           in1=flat(at(("ft", unit))), op0=ALU.mult, op1=ALU.mult)
             if j == NJ - 1:
-                give(("ft", k))
+                give(("ft", unit))
 
-        def turn_gradient(k, half):
-            bank = take(("gt", k, half), [P, 2, 2, P], F32)
-            for jj in range(2):
-                words = get("gm%d" % (2 * half + jj), k)[:].bitcast(F32)
+        def turn_gradient(unit, half):
+            bank = take(("gt", unit, half), [P, 2, 2, P], F32)
+            for j0 in range(2):
+                words = get("gm%d" % (2 * half + j0), unit)[:].bitcast(F32)
                 for h in range(2):
-                    nc.tensor.transpose(bank[:, jj, h, :], block(words, h), ident[:])
+                    nc.tensor.transpose(bank[:, j0, h, :], block(words, h), ident[:])
 
-        def copy_gradient(k, half):
-            gt = new("gt", k, [P, 2, 2, P, 2], F32, 1, 64) if half == 0 else get("gt", k)
-            nc.scalar.copy(out=gt[:, half], in_=at(("gt", k, half))[:].rearrange("p j h n -> p j n h"))
-            give(("gt", k, half))
+        def copy_gradient(unit, half):
+            gt = new("gt", unit, [P, 2, 2, P, 2], F32, 1, 64) if half == 0 else get("gt", unit)
+            nc.scalar.copy(out=gt[:, half], in_=at(("gt", unit, half))[:].rearrange("p j0 h m -> p j0 m h"))
+            give(("gt", unit, half))
 
         gq = {}
 
-        def quantise_gm(k):
-            gq[k] = quantise("gq", get("gt", k)[:].rearrange("p a j n h -> p (a j n h)").bitcast(BF16), 3)
+        def quantise_gm(unit):
+            gq[unit] = quantise("gq", get("gt", unit)[:].rearrange("p j1 j0 m h -> p (j1 j0 m h)").bitcast(BF16), 4)
 
-        def out_pass(c, n, gi):
-            bank = take(("out", c, n), [P, KP], F32) if gi == 0 else at(("out", c, n))
-            mx(bank[:], xuq[gi], n * P, gq[c * NG + gi], 0, KP, gi == 0, gi == NG - 1)
+        def out_pass(chunk, n, group):
+            bank = take(("out", chunk, n), [P, KP], F32) if group == 0 else at(("out", chunk, n))
+            mx(bank[:], xuq[group], n * P, gq[chunk * GROUPS + group], 0, KP, group == 0, group == GROUPS - 1)
 
-        def out_copy(c, n, on_vector):
-            res = work.tile([P, NI * NJ, OC], F32, name="res", bufs=4)
+        def out_mm(chunk, n):
+            for group in range(GROUPS):
+                out_pass(chunk, n, group)
+
+        def out_copy(on_vector, chunk, n):
+            res = work.tile([P, EXPERTS, OC], F32, name="res", bufs=ROW_TILES)
             dst = res[:].rearrange("p (i j) o -> p i j o", i=NI)
-            src = at(("out", c, n))[:].rearrange("p (j i o) -> p i j o", j=NJ, i=NI)
+            src = at(("out", chunk, n))[:].rearrange("p (j i o) -> p i j o", j=NJ, i=NI)
             if on_vector:
                 nc.vector.tensor_scalar(out=dst, in0=src, scalar1=0.125, scalar2=None, op0=ALU.mult)
             else:
                 nc.scalar.activation(out=dst, in_=src, func=ACT.Copy, scale=0.125)
-            give(("out", c, n))
-            dst = out[n * P:(n + 1) * P].rearrange("d i j o -> d (i j) o")[:, :, c * OC:(c + 1) * OC]
+            give(("out", chunk, n))
             queue = nc.scalar if on_vector else nc.sync
-            queue.dma_start(out=dst, in_=res[:])
-
-        def weighted_x(gi):
-            weigh_x(gi)
-            for n in range(D // P):
-                interleave_x(True, gi, n)
-            quantise_xu(gi)
+            queue.dma_start(out=out[n * P:(n + 1) * P].rearrange("d i j o -> d (i j) o")[:, :, chunk * OC:(chunk + 1) * OC], in_=res[:])
 
         nc.vector.tensor_scalar(out=wsn[:], in0=ws[:], scalar1=-1.0, scalar2=None, op0=ALU.mult)
-        widen(False, wide_mu, wb_mu[0][:, 1], ws, 1)
-        widen(True, wide_mu, wb_mu[0][:, 0], ws, 0)
-        turn_x(0, 0)
-        turn_x(0, 1)
-        copy_x(0, 0)
-        copy_x(0, 1)
-        widen(True, wide_mu, wb_mu[1][:, 0], ws, 2)
-        widen(True, wide_mu, wb_mu[1][:, 1], ws, 3)
-        spread_y(0)
+        widen(ON_SCALAR, "mu", wb_mu[0][:, 1], ws, 1)
+        widen(ON_VECTOR, "mu", wb_mu[0][:, 0], ws, 0)
+        for h in range(2):
+            turn_x(0, h)
+        for h in range(2):
+            copy_x(0, h)
+        for t in (2, 3):
+            widen(ON_VECTOR, "mu", wb_mu[1][:, t - 2], ws, t)
+        for t in (0, 1):
+            widen(ON_SCALAR, "c", wb_c[0][:, t], ws, t)
         gain_x(0)
+        widen(ON_VECTOR, "c", wb_c[1][:, 0], ws, 2)
+        quantise_xg(0)
+        widen(ON_VECTOR, "c", wb_c[1][:, 1], ws, 3)
+        spread_y(0)
         variance_columns()
         turn_y(0)
-        widen(False, wide_c, wb_c[:, 0], ws, 0)
-        copy_y(0)
         for j in range(NJ):
-            interleave(True, 0, "mu", j)
-        quantise_xg(0)
-        widen(False, wide_c, wb_c[:, 1], ws, 1)
-        quantise_w(0, "mu")
-        widen(True, wide_c, wb_c[:, 2], ws, 2)
-        widen(True, wide_c, wb_c[:, 3], ws, 3)
-        turn_x(1, 0)
-        turn_x(1, 1)
-        copy_x(1, 0)
-        copy_x(1, 1)
-        for t in range(PACK):
-            widen(False, wide_a, wb_a[:, t], wsn, t)
-        for j in range(1, NJ):
-            interleave(True, 0, "c", j)
-        interleave(True, 0, "c", 0)
-        gain_x(1)
+            interleave(ON_VECTOR, 0, "c", j)
+        interleave(ON_VECTOR, 0, "mu", 0)
         quantise_w(0, "c")
-        interleave(False, 0, "a", 0)
+        for j in range(1, NJ):
+            interleave(ON_VECTOR, 0, "mu", j)
+        for h in range(2):
+            turn_x(1, h)
+        for h in range(2):
+            copy_x(1, h)
+        for t in range(PACK):
+            widen(ON_SCALAR, "a", wb_a[:, t], wsn, t)
+        gain_x(1)
+        quantise_w(0, "mu")
+        interleave(ON_VECTOR, 0, "a", 0)
         quantise_xg(1)
-        weighted_x(0)
         quantise_w(0, "a")
 
-        def early(k):
-            c = k // NG + 1
-            if c < NC:
-                quantise_w(c, ("c", "mu")[k % NG])
+        def next_chunk(unit):
+            return unit // GROUPS + 1
 
-        def early_rest(k):
-            c = k // NG + 1
-            if c < NC and k % NG == 0:
-                spread_y(c)
-            if c < NC and k % NG == 1:
-                quantise_w(c, "a")
+        def next_kind(unit):
+            return ("c", "mu")[unit % GROUPS]
 
-        def next_weights(k, j):
-            c = k // NG + 1
-            if c < NC:
-                interleave(j == 3, c, ("c", "mu")[k % NG], j)
+        def next_weights(unit, j):
+            if next_chunk(unit) < CHUNKS:
+                interleave(j == NJ - 1, next_chunk(unit), next_kind(unit), j)
 
-        def next_rest(k):
-            c = k // NG + 1
-            if c < NC and k % NG == 0:
-                interleave(False, c, "a", 0)
-                turn_y(c)
-                copy_y(c)
-            if k == 0:
+        def next_codes(unit):
+            if next_chunk(unit) < CHUNKS:
+                quantise_w(next_chunk(unit), next_kind(unit))
+
+        def next_small_vector(unit):
+            if next_chunk(unit) < CHUNKS:
+                if unit % GROUPS == 0:
+                    spread_y(next_chunk(unit))
+                else:
+                    quantise_w(next_chunk(unit), "a")
+
+        def next_small_scalar(unit):
+            if next_chunk(unit) < CHUNKS and unit % GROUPS == 0:
+                interleave(ON_SCALAR, next_chunk(unit), "a", 0)
+                turn_y(next_chunk(unit))
+            if unit == 0:
                 q_columns()
 
-        def late(k):
-            if k == 0:
-                weighted_x(1)
+        def first_weigh_x(unit, group):
+            if unit == 0:
+                weigh_x(group)
 
-        last = UNITS - 1
+        def first_quantise_xu(unit):
+            if unit < GROUPS:
+                quantise_xu(unit)
 
-        def when(k, step, *args):
-            if 0 <= k <= last:
-                step(k, *args)
+        def when(unit, step, *args):
+            if 0 <= unit <= LAST:
+                step(unit, *args)
 
-        def out_rows(k, slot):
-            c, later = divmod(k - 4, NG)
-            if not 0 <= c < NC - 1:
-                return []
-            if c == NC - 2:
-                return [(c, 2 * slot), (c, 2 * slot + 1)] if later == 0 else []
-            return [(c, 2 * later + slot)]
+        def out_tile(iteration, slot):
+            chunk, later = divmod(iteration - (GROUPS + 2), GROUPS)
+            return (chunk, 2 * later + slot) if 0 <= chunk < CHUNKS - 2 else None
 
-        def out_product(k, slot):
-            for c, n in out_rows(k, slot):
-                for gi in range(NG):
-                    out_pass(c, n, gi)
+        def out_product(iteration, slot):
+            if out_tile(iteration, slot):
+                out_mm(*out_tile(iteration, slot))
 
-        def out_store(k, slot):
-            for c, n in out_rows(k, slot):
-                out_copy(c, n, False)
+        def out_store(iteration, slot):
+            if out_tile(iteration, slot):
+                out_copy(ON_SCALAR, *out_tile(iteration, slot))
 
-        def out_open(k):
-            if k == last:
-                for n in range(D // P):
-                    out_pass(k // NG, n, 0)
+        for iteration in range(-1, UNITS):
+            ahead, cur, mid, old = iteration + 1, iteration, iteration - 1, iteration - 2
+            when(mid, shift)
+            when(mid, arg_mm, 0)
+            when(cur, residual, 0)
+            when(cur, max_123)
+            when(mid, exp_arg, 0)
+            when(mid, arg_mm, 1)
+            when(cur, square, 0)
+            when(cur, residual, 1)
+            when(cur, gap_j, 1)
+            when(mid, product, 0)
+            when(mid, exp_arg, 1)
+            when(cur, mu_mm, 2)
+            when(cur, mu_mm, 3)
+            when(mid, arg_mm, 2)
+            when(cur, square, 1)
+            when(cur, residual, 2)
+            when(cur, gap_j, 2)
+            when(mid, product, 1)
+            when(mid, exp_arg, 2)
+            when(cur, cost_mm, 0)
+            when(mid, arg_mm, 3)
+            when(cur, square, 2)
+            when(cur, residual, 3)
+            when(cur, gap_j, 3)
+            when(mid, product, 2)
+            when(cur, cost_copy, 0)
+            when(mid, exp_arg, 3)
+            when(cur, cost_mm, 1)
+            when(cur, square, 3)
+            when(old, gradient, 0)
+            when(old, gradient, 1)
+            when(mid, product, 3)
+            when(cur, cost_copy, 1)
+            when(mid, sum_e)
+            when(cur, exp_gap, 0)
+            when(old, gradient, 2)
+            when(old, gradient, 3)
+            when(cur, cost_mm, 2)
+            when(old, turn_gradient, 0)
+            when(cur, cost_copy, 2)
+            when(cur, cost_mm, 3)
+            when(old, copy_gradient, 0)
+            when(old, turn_gradient, 1)
+            when(cur, first_weigh_x, 0)
+            when(cur, min_pair, 0)
+            when(cur, first_quantise_xu)
+            when(mid, weigh_sums)
+            when(cur, next_weights, 3)
+            when(mid, total_i1)
+            when(cur, next_codes)
+            when(mid, total_i0)
+            when(cur, next_small_vector)
+            when(cur, cost_copy, 3)
+            when(old, copy_gradient, 1)
+            when(cur, a_mm)
+            when(ahead, d_mm, 1)
+            when(cur, exp_gap, 1)
+            out_product(iteration, 0)
+            when(mid, invert)
+            when(cur, min_pair, 1)
+            when(mid, weigh_q)
+            when(cur, min_j)
+            when(mid, factor)
+            when(cur, add_a)
+            when(ahead, d1_copy)
+            when(cur, next_small_scalar)
+            when(ahead, d_mm, 2)
+            when(cur, sum_s)
+            out_store(iteration, 0)
+            when(cur, s_copy)
+            out_product(iteration, 1)
+            when(old, quantise_gm)
+            when(cur, min_i1)
+            when(ahead, max_12)
+            when(cur, min_i0)
+            when(cur, first_weigh_x, 1)
+            when(ahead, next_weights, 0)
+            when(ahead, next_weights, 1)
+            when(mid, turn_factor)
+            when(ahead, d_mm, 3)
+            out_store(iteration, 1)
+            when(ahead, mu_mm, 0)
+            when(ahead, mu_mm, 1)
+            when(ahead, next_weights, 2)
+            when(cur, pair)
+            when(cur, cofactor)
 
-        for k in range(-1, UNITS + 2):
-            n, a, b, c = k + 1, k, k - 1, k - 2
-            when(b, shift)
-            when(b, arg_mm, 0)
-            when(a, residual, 0)
-            when(a, max_b)
-            when(b, exp_arg, 0)
-            when(b, arg_mm, 1)
-            when(a, square, 0)
-            when(a, residual, 1)
-            when(a, gap_j, 1)
-            when(b, product, 0)
-            when(b, exp_arg, 1)
-            when(a, mu_mm, 2)
-            when(a, mu_mm, 3)
-            when(b, arg_mm, 2)
-            when(a, square, 1)
-            when(a, residual, 2)
-            when(a, gap_j, 2)
-            when(b, product, 1)
-            when(b, exp_arg, 2)
-            when(a, cost_mm, 0)
-            when(b, arg_mm, 3)
-            when(a, square, 2)
-            when(a, residual, 3)
-            when(a, gap_j, 3)
-            when(b, product, 2)
-            when(a, cost_copy, 0)
-            when(b, exp_arg, 3)
-            when(a, cost_mm, 1)
-            when(a, square, 3)
-            when(c, gradient, 0)
-            when(c, gradient, 1)
-            when(b, product, 3)
-            when(a, cost_copy, 1)
-            when(b, sum_t)
-            when(a, exp_gap, 0)
-            when(c, gradient, 2)
-            when(c, gradient, 3)
-            when(a, cost_mm, 2)
-            when(c, turn_gradient, 0)
-            when(a, cost_copy, 2)
-            when(a, cost_mm, 3)
-            when(c, copy_gradient, 0)
-            when(c, turn_gradient, 1)
-            when(a, late)
-            when(a, min_pair, 0)
-            when(b, weigh_t)
-            when(a, next_weights, 3)
-            when(b, total_a)
-            when(a, early)
-            when(b, total_b)
-            when(a, early_rest)
-            when(a, cost_copy, 3)
-            when(c, copy_gradient, 1)
-            when(a, a_mm)
-            when(n, d_mm, 1)
-            when(a, exp_gap, 1)
-            out_product(k, 0)
-            when(b, invert)
-            when(a, min_pair, 1)
-            when(b, weigh_q)
-            when(a, min_j)
-            when(b, factor)
-            when(a, add_a)
-            when(n, d1_copy)
-            when(a, next_rest)
-            when(n, d_mm, 2)
-            when(a, sum_s)
-            out_store(k, 0)
-            when(a, s_copy)
-            out_product(k, 1)
-            when(c, quantise_gm)
-            when(a, min_i_a)
-            when(n, max_a)
-            when(a, min_i_b)
-            when(n, next_weights, 0)
-            when(n, next_weights, 1)
-            when(b, turn_factor)
-            when(b, out_open)
-            when(n, d_mm, 3)
-            out_store(k, 1)
-            when(n, mu_mm, 0)
-            when(n, mu_mm, 1)
-            when(n, next_weights, 2)
-            when(a, pair)
-            when(a, cofactor)
-        for n in range(D // P):
-            out_pass(NC - 1, n, NG - 1)
-        for n in range(D // P):
-            out_copy(NC - 1, n, n % 2 == 1)
+        mid, old = LAST, LAST - 1
+        for n in range(2):
+            out_mm(CHUNKS - 2, n)
+        shift(mid)
+        for half in range(2):
+            arg_mm(mid, half)
+            gradient(old, 2 * half)
+            gradient(old, 2 * half + 1)
+            exp_arg(mid, half)
+        for j in range(2, NJ):
+            arg_mm(mid, j)
+            product(mid, j - 2)
+            exp_arg(mid, j)
+        for half in range(2):
+            turn_gradient(old, half)
+        product(mid, 2)
+        sum_e(mid)
+        for half in range(2):
+            copy_gradient(old, half)
+        for n in range(2):
+            out_copy(ON_SCALAR, CHUNKS - 2, n)
+        for n in range(2, ROW_TILES):
+            out_mm(CHUNKS - 2, n)
+            out_copy(ON_SCALAR, CHUNKS - 2, n)
+        product(mid, 3)
+        weigh_sums(mid)
+        quantise_gm(old)
+        total_i1(mid)
+        total_i0(mid)
+        invert(mid)
+        weigh_q(mid)
+        factor(mid)
+        turn_factor(mid)
+        for half in range(2):
+            gradient(mid, 2 * half)
+            gradient(mid, 2 * half + 1)
+            turn_gradient(mid, half)
+            copy_gradient(mid, half)
+        for n in range(ROW_TILES):
+            out_pass(CHUNKS - 1, n, 0)
+        quantise_gm(mid)
+        for n in range(ROW_TILES):
+            out_pass(CHUNKS - 1, n, GROUPS - 1)
+        for n in range(ROW_TILES):
+            out_copy(n % 2 == 1, CHUNKS - 1, n)

@@ -171,16 +171,23 @@ def tile_hierarchicalmixtureeffectiveweightgradie_kernel(tc, x, g, w_bytes, w_sc
         def quantise_xg(group):
             xq[group] = quantise("xq", x_gained[group][:].rearrange("d col t -> d (col t)"), GROUPS)
 
+        u32 = keep.tile([P, GROUPS, PACK], F32, name="u32")
+        x_scaled = {}
         x_weighed = {}
         xuq = {}
 
-        def weigh_x(group):
-            rows = work.tile([P, PACK, D], BF16, name="xt")
-            for t in range(PACK):
-                nc.vector.tensor_scalar(out=rows[:, t], in0=x_sb[group][:, t], scalar1=u_sb[:, group, t:t + 1], scalar2=None, op0=ALU.mult)
-            x_weighed[group] = work.tile([P, D, PACK], BF16, name="xgrp", bufs=2, align_bytes=64)
-            nc.vector.tensor_copy(out=x_weighed[group][:].rearrange("p (a b) t -> p a t b", b=RUN),
-                                  in_=rows[:].rearrange("p t (a b) -> p a t b", b=RUN))
+        def weigh_x(group, half):
+            if half == 0:
+                x_scaled[group] = work.tile([P, PACK, D], BF16, name="xt")
+            for t in (2 * half, 2 * half + 1):
+                nc.scalar.activation(out=x_scaled[group][:, t], in_=x_sb[group][:, t], func=ACT.Copy, scale=u32[:, group, t:t + 1])
+
+        def interleave_x(group, half):
+            if half == 0:
+                x_weighed[group] = work.tile([P, D, PACK], BF16, name="xgrp", bufs=2, align_bytes=64)
+            cols = slice(half * D // 2, (half + 1) * D // 2)
+            nc.scalar.copy(out=x_weighed[group][:, cols].rearrange("p (a b) t -> p a t b", b=RUN),
+                           in_=x_scaled[group][:, :, cols].rearrange("p t (a b) -> p a t b", b=RUN))
 
         def quantise_xu(group):
             xuq[group] = quantise("xuq", x_weighed[group][:].rearrange("p d t -> p (d t)"), GROUPS)
@@ -456,6 +463,10 @@ def tile_hierarchicalmixtureeffectiveweightgradie_kernel(tc, x, g, w_bytes, w_sc
         widen(ON_VECTOR, "c", wb_c[1][:, 1], ws, 3)
         spread_y(0)
         variance_columns()
+        for h in range(2):
+            turn_x(1, h)
+        for h in range(2):
+            copy_x(1, h)
         turn_y(0)
         for j in range(NJ):
             interleave(ON_VECTOR, 0, "c", j)
@@ -463,17 +474,7 @@ def tile_hierarchicalmixtureeffectiveweightgradie_kernel(tc, x, g, w_bytes, w_sc
         quantise_w(0, "c")
         for j in range(1, NJ):
             interleave(ON_VECTOR, 0, "mu", j)
-        for h in range(2):
-            turn_x(1, h)
-        for h in range(2):
-            copy_x(1, h)
-        for t in range(PACK):
-            widen(ON_SCALAR, "a", wb_a[:, t], wsn, t)
-        gain_x(1)
         quantise_w(0, "mu")
-        interleave(ON_VECTOR, 0, "a", 0)
-        quantise_xg(1)
-        quantise_w(0, "a")
 
         def next_chunk(unit):
             return unit // GROUPS + 1
@@ -503,13 +504,25 @@ def tile_hierarchicalmixtureeffectiveweightgradie_kernel(tc, x, g, w_bytes, w_sc
             if unit == 0:
                 q_columns()
 
-        def first_weigh_x(unit, group):
-            if unit == 0:
-                weigh_x(group)
+        def token_weights(unit, half):
+            if unit < 2 * GROUPS:
+                (weigh_x, interleave_x)[unit % 2](unit // 2, half)
 
-        def first_quantise_xu(unit):
-            if unit < GROUPS:
-                quantise_xu(unit)
+        def token_codes(unit):
+            if unit < 2 * GROUPS and unit % 2 == 1:
+                quantise_xu(unit // 2)
+
+        def first_gate_row(unit, t):
+            if unit == 0:
+                widen(ON_SCALAR, "a", wb_a[:, t], wsn, t)
+
+        def head_rest(unit):
+            if unit == 0:
+                gain_x(1)
+                interleave(ON_VECTOR, 0, "a", 0)
+                quantise_xg(1)
+                quantise_w(0, "a")
+                nc.vector.tensor_copy(out=u32[:], in_=u_sb[:])
 
         def when(unit, step, *args):
             if 0 <= unit <= LAST:
@@ -536,6 +549,7 @@ def tile_hierarchicalmixtureeffectiveweightgradie_kernel(tc, x, g, w_bytes, w_sc
             when(mid, exp_arg, 0)
             when(mid, arg_mm, 1)
             when(cur, square, 0)
+            when(cur, first_gate_row, 0)
             when(cur, residual, 1)
             when(cur, gap_j, 1)
             when(mid, product, 0)
@@ -544,6 +558,7 @@ def tile_hierarchicalmixtureeffectiveweightgradie_kernel(tc, x, g, w_bytes, w_sc
             when(cur, mu_mm, 3)
             when(mid, arg_mm, 2)
             when(cur, square, 1)
+            when(cur, first_gate_row, 1)
             when(cur, residual, 2)
             when(cur, gap_j, 2)
             when(mid, product, 1)
@@ -551,6 +566,7 @@ def tile_hierarchicalmixtureeffectiveweightgradie_kernel(tc, x, g, w_bytes, w_sc
             when(cur, cost_mm, 0)
             when(mid, arg_mm, 3)
             when(cur, square, 2)
+            when(cur, first_gate_row, 2)
             when(cur, residual, 3)
             when(cur, gap_j, 3)
             when(mid, product, 2)
@@ -558,12 +574,14 @@ def tile_hierarchicalmixtureeffectiveweightgradie_kernel(tc, x, g, w_bytes, w_sc
             when(mid, exp_arg, 3)
             when(cur, cost_mm, 1)
             when(cur, square, 3)
+            when(cur, first_gate_row, 3)
             when(old, gradient, 0)
             when(old, gradient, 1)
             when(mid, product, 3)
             when(cur, cost_copy, 1)
             when(mid, sum_e)
             when(cur, exp_gap, 0)
+            when(mid, token_weights, 1)
             when(old, gradient, 2)
             when(old, gradient, 3)
             when(cur, cost_mm, 2)
@@ -572,9 +590,9 @@ def tile_hierarchicalmixtureeffectiveweightgradie_kernel(tc, x, g, w_bytes, w_sc
             when(cur, cost_mm, 3)
             when(old, copy_gradient, 0)
             when(old, turn_gradient, 1)
-            when(cur, first_weigh_x, 0)
+            when(cur, head_rest)
             when(cur, min_pair, 0)
-            when(cur, first_quantise_xu)
+            when(mid, token_codes)
             when(mid, weigh_sums)
             when(cur, next_weights, 3)
             when(mid, total_i1)
@@ -594,6 +612,7 @@ def tile_hierarchicalmixtureeffectiveweightgradie_kernel(tc, x, g, w_bytes, w_sc
             when(mid, factor)
             when(cur, add_a)
             when(ahead, d1_copy)
+            when(cur, token_weights, 0)
             when(cur, next_small_scalar)
             when(ahead, d_mm, 2)
             when(cur, sum_s)
@@ -604,7 +623,6 @@ def tile_hierarchicalmixtureeffectiveweightgradie_kernel(tc, x, g, w_bytes, w_sc
             when(cur, min_i1)
             when(ahead, max_12)
             when(cur, min_i0)
-            when(cur, first_weigh_x, 1)
             when(ahead, next_weights, 0)
             when(ahead, next_weights, 1)
             when(mid, turn_factor)
@@ -644,6 +662,8 @@ def tile_hierarchicalmixtureeffectiveweightgradie_kernel(tc, x, g, w_bytes, w_sc
         weigh_sums(mid)
         quantise_gm(old)
         total_i1(mid)
+        for n in range(2):
+            out_pass(CHUNKS - 1, n, 0)
         total_i0(mid)
         invert(mid)
         weigh_q(mid)
@@ -654,7 +674,7 @@ def tile_hierarchicalmixtureeffectiveweightgradie_kernel(tc, x, g, w_bytes, w_sc
             gradient(mid, 2 * half + 1)
             turn_gradient(mid, half)
             copy_gradient(mid, half)
-        for n in range(ROW_TILES):
+        for n in range(2, ROW_TILES):
             out_pass(CHUNKS - 1, n, 0)
         quantise_gm(mid)
         for n in range(ROW_TILES):

import math
from contextlib import ExitStack

import concourse.mybir as mybir
from concourse.masks import make_identity

T, D, NI, NJ, O = 1024, 512, 4, 4, 128
FLOPS = 2 * T * D * 36 * O + 2 * D * T * NI * NJ * O

F32 = mybir.dt.float32
BF16 = mybir.dt.bfloat16
U32 = mybir.dt.uint32
U8 = mybir.dt.uint8
FP8 = mybir.dt.float8_e4m3fn
X4 = mybir.dt.float8_e4m3fn_x4
ALU = mybir.AluOpType
ACT = mybir.ActivationFunctionType

P = 128
PACK = 4
KP = P * PACK
BLOCKS = KP // P
GROUPS = T // KP
OC = P // NI
CHUNKS = O // OC
UNITS = CHUNKS * GROUPS
LAST = UNITS - 1
ROW_TILES = D // P
EXPERTS = NI * NJ
BANKS = 8
RUN = 4
ON_VECTOR, ON_SCALAR = True, False


def tile_hierarchicalmixtureeffectiveweightgradie_kernel(tc, x, g, w_bytes, w_scale, y, s, u, q, out):
    nc = tc.nc
    with ExitStack() as ctx:
        keep = ctx.enter_context(tc.tile_pool(name="keep", bufs=1))
        work = ctx.enter_context(tc.tile_pool(name="work", bufs=1))
        psum = ctx.enter_context(tc.psum_pool(name="psum", bufs=1))
        ctx.enter_context(tc.manual_schedule())

        free_banks = list(range(BANKS))
        held = {}

        def take(key, shape, dtype):
            index = free_banks[0]
            free_banks.remove(index)
            bank = psum.tile(shape, dtype, name="bank%d" % index)
            held[key] = (index, bank)
            return bank

        def give(key):
            free_banks.append(held[key][0])

        def at(key):
            return held[key][1]

        w_rows = w_bytes.rearrange("(p t) m o -> p t m o", t=PACK)
        ws = keep.tile([P, PACK], F32, name="ws")
        nc.sync.dma_start(out=ws[:], in_=w_scale.rearrange("(p t) a b -> p (t a b)", t=PACK))
        g4 = keep.tile([P, PACK], BF16, name="g4")
        nc.sync.dma_start(out=g4[:], in_=g.rearrange("(p t) -> p t", t=PACK))

        def load_bytes(tile, t0, t1, m0, m1):
            nc.sync.dma_start(out=tile[:], in_=w_rows[:, t0:t1, m0:m1, :].rearrange("p t m o -> p t (m o)"))

        x_sb = [keep.tile([P, PACK, D], BF16, name="x_sb%d" % group) for group in range(GROUPS)]
        x_rows = x.rearrange("(g p t) d -> g p t d", p=P, t=PACK)
        wb_mu = [keep.tile([P, 2, EXPERTS * O], U8, name="wb_mu%d" % part) for part in range(2)]
        wb_c = [keep.tile([P, 2, EXPERTS * O], U8, name="wb_c%d" % part) for part in range(2)]
        load_bytes(wb_mu[0], 0, 2, 0, EXPERTS)
        nc.sync.dma_start(out=x_sb[0][:], in_=x_rows[0])
        load_bytes(wb_mu[1], 2, 4, 0, EXPERTS)
        load_bytes(wb_c[0], 0, 2, EXPERTS, 2 * EXPERTS)
        load_bytes(wb_c[1], 2, 4, EXPERTS, 2 * EXPERTS)
        y_sb = keep.tile([P, GROUPS, PACK, O], BF16, name="y_sb")
        nc.sync.dma_start(out=y_sb[:], in_=y.rearrange("(g p t) o -> p g t o", p=P, t=PACK))
        s_rows = keep.tile([P, P], BF16, name="s_rows")
        nc.gpsimd.memset(s_rows[:], 0.0)
        nc.sync.dma_start(out=s_rows[0:NJ * CHUNKS, :].rearrange("r (i o) -> r i o", i=NI),
                          in_=s.rearrange("i j (c o) -> (j c) i o", o=OC))
        wb_a = keep.tile([P, PACK, NI * O], U8, name="wb_a")
        load_bytes(wb_a, 0, PACK, 2 * EXPERTS, 2 * EXPERTS + NI)
        nc.sync.dma_start(out=x_sb[1][:], in_=x_rows[1])
        q_rows = keep.tile([P, 2, P], BF16, name="q_rows")
        nc.gpsimd.memset(q_rows[:], 0.0)
        for h in range(2):
            nc.sync.dma_start(out=q_rows[0:2 * GROUPS, h, :].rearrange("r (p e) -> r p e", e=2),
                              in_=q.rearrange("(r p h e) -> h r p e", p=P // 2, h=2, e=2)[h])
        u_sb = keep.tile([P, GROUPS, PACK], BF16, name="u_sb")
        nc.sync.dma_start(out=u_sb[:], in_=u.rearrange("(g p t) -> p g t", p=P, t=PACK))

        ident = keep.tile([P, P], F32, name="ident")
        make_identity(nc, ident[:])
        ident_bf = keep.tile([P, P], BF16, name="ident_bf")
        make_identity(nc, ident_bf[:])

        wsn = keep.tile([P, PACK], F32, name="wsn")
        wide = {
            "mu": keep.tile([P, PACK, NI, NJ, O], BF16, name="wide_mu"),
            "c": keep.tile([P, PACK, NI, NJ, O], BF16, name="wide_c"),
            "a": keep.tile([P, PACK, NI, 1, O], BF16, name="wide_a"),
        }

        def widen(on_vector, kind, codes_in, scale, t):
            dst = wide[kind][:, t].rearrange("p i j o -> p (i j o)")
            if on_vector:
                nc.vector.tensor_scalar(out=dst, in0=codes_in.bitcast(FP8), scalar1=scale[:, t:t + 1], scalar2=None, op0=ALU.mult)
            else:
                nc.scalar.activation(out=dst, in_=codes_in.bitcast(FP8), func=ACT.Copy, scale=scale[:, t:t + 1])

        wq = {}
        grouped = {}

        def interleave(on_vector, chunk, kind, j):
            if (chunk, kind) not in grouped:
                grouped[(chunk, kind)] = work.tile([P, wide[kind].shape[3], NI, OC, PACK], BF16, name="grp_" + kind, align_bytes=64)
            src = wide[kind][:, :, :, j, chunk * OC:(chunk + 1) * OC]
            dst = grouped[(chunk, kind)][:, j]
            if kind == "c" and j == 0:
                src = src.rearrange("p t i o -> p i o t")
                if on_vector:
                    nc.vector.tensor_scalar(out=dst, in0=src, scalar1=-1.0, scalar2=None, op0=ALU.mult)
                else:
                    nc.scalar.activation(out=dst, in_=src, func=ACT.Copy, scale=-1.0)
                return
            src = src.rearrange("p t i (a b) -> p i a t b", b=RUN)
            dst = dst.rearrange("p i (a b) t -> p i a t b", b=RUN)
            if on_vector:
                nc.vector.tensor_copy(out=dst, in_=src)
            else:
                nc.scalar.copy(out=dst, in_=src)

        def quantise(name, src, bufs):
            width = src.shape[1] // PACK
            codes = work.tile([P, width], U32, name=name + "_codes", bufs=bufs, align_bytes=64)
            scales = work.tile([P, width], U8, name=name + "_scales", bufs=bufs, align_bytes=64)
            nc.vector.quantize_mx(out=codes[:].bitcast(X4), scales=scales[:], in_=src)
            return codes, scales

        def quantise_w(chunk, kind):
            wq[(chunk, kind)] = quantise("wq_" + kind, grouped[(chunk, kind)][:].rearrange("p j i o t -> p (j i o t)"), 2)

        def mx(dst, lhs, l0, rhs, r0, width, start, stop):
            nc.tensor.matmul_mx(out=dst, lhsT=lhs[0][:, l0:l0 + P].bitcast(X4), lhsT_scale=lhs[1][:, l0:l0 + P],
                                rhs=rhs[0][:, r0:r0 + width].bitcast(X4), rhs_scale=rhs[1][:, r0:r0 + width], start=start, stop=stop)

        x_turned = {}
        x_gained = {}
        xq = {}

        def turn_x(group, h):
            words = x_sb[group][:].bitcast(F32)
            bank = take(("xt", group, h), [P, 2, 2, P], F32)
            for e in range(2):
                for w in range(2):
                    nc.tensor.transpose(bank[:, e, w, :], words[:, 2 * h + e, w::2], ident[:])

        def copy_x(group, h):
            if group not in x_turned:
                x_turned[group] = work.tile([P, 2, P, PACK], F32, name="xt")
            nc.scalar.copy(out=x_turned[group][:, h], in_=at(("xt", group, h))[:].rearrange("d e w p -> d p (e w)"))
            give(("xt", group, h))

        def gain_x(group):
            x_gained[group] = work.tile([P, KP, PACK], BF16, name="xgrp", bufs=2, align_bytes=64)
            src = x_turned[group][:].rearrange("d h p w -> d (h p w)").bitcast(BF16).rearrange("d (col t) -> d col t", t=PACK)
            nc.vector.tensor_tensor(out=x_gained[group][:], in0=src, in1=g4[:].unsqueeze(1).broadcast_to([P, KP, PACK]), op=ALU.mult)

        def quantise_xg(group):
            xq[group] = quantise("xq", x_gained[group][:].rearrange("d col t -> d (col t)"), GROUPS)

        u32 = keep.tile([P, GROUPS, PACK], F32, name="u32")
        x_scaled = {}
        x_weighed = {}
        xuq = {}

        def weigh_x(group, half):
            if half == 0:
                x_scaled[group] = work.tile([P, PACK, D], BF16, name="xt")
            for t in (2 * half, 2 * half + 1):
                nc.scalar.activation(out=x_scaled[group][:, t], in_=x_sb[group][:, t], func=ACT.Copy, scale=u32[:, group, t:t + 1])

        def interleave_x(group, half):
            if half == 0:
                x_weighed[group] = work.tile([P, D, PACK], BF16, name="xgrp", bufs=2, align_bytes=64)
            cols = slice(half * D // 2, (half + 1) * D // 2)
            nc.scalar.copy(out=x_weighed[group][:, cols].rearrange("p (a b) t -> p a t b", b=RUN),
                           in_=x_scaled[group][:, :, cols].rearrange("p t (a b) -> p a t b", b=RUN))

        def quantise_xu(group):
            xuq[group] = quantise("xuq", x_weighed[group][:].rearrange("p d t -> p (d t)"), GROUPS)

        y_spread = {}
        y_turned = {}

        def spread_y(chunk):
            y_spread[chunk] = work.tile([P, GROUPS * PACK, NI, OC], BF16, name="yrep")
            src = y_sb[:].rearrange("p g t o -> p (g t) o")[:, :, chunk * OC:(chunk + 1) * OC]
            nc.vector.tensor_copy(out=y_spread[chunk][:], in_=src.unsqueeze(2).broadcast_to([P, GROUPS * PACK, NI, OC]))

        def turn_y(chunk):
            bank = take(("yt", chunk), [P, GROUPS * PACK, P], BF16)
            for row in range(GROUPS * PACK):
                nc.tensor.transpose(bank[:, row, :], y_spread[chunk][:, row].rearrange("p i o -> p (i o)"), ident_bf[:])
            y_turned[chunk] = work.tile([P, GROUPS, KP], BF16, name="yt", bufs=2)
            nc.scalar.copy(out=y_turned[chunk][:].rearrange("m g (h p e) -> m (g h) p e", h=2, e=2),
                           in_=bank[:].rearrange("m (gh e) p -> m gh p e", e=2))
            give(("yt", chunk))

        var = keep.tile([P, NJ * CHUNKS], F32, name="var")
        root = keep.tile([P, NJ * CHUNKS], F32, name="root")
        half_root = keep.tile([P, NJ * CHUNKS], F32, name="half_root")
        half_s = keep.tile([P, NJ * CHUNKS], F32, name="half_s")

        def variance_columns():
            bank = take("st", [P, P], BF16)
            nc.tensor.transpose(bank[:], s_rows[:], ident_bf[:])
            nc.scalar.activation(out=var[:], in_=bank[:, 0:NJ * CHUNKS], func=ACT.Exp, scale=-1.0)
            nc.scalar.activation(out=root[:], in_=bank[:, 0:NJ * CHUNKS], func=ACT.Exp, scale=-0.5)
            nc.scalar.activation(out=half_s[:], in_=bank[:, 0:NJ * CHUNKS], func=ACT.Copy, scale=-0.5)
            nc.scalar.activation(out=half_root[:], in_=root[:], func=ACT.Copy, scale=math.sqrt(0.5))
            give("st")

        def column(tile, unit, j):
            index = j * CHUNKS + unit // GROUPS
            return tile[:, index:index + 1]

        q_col = keep.tile([P, GROUPS, 2, 2], F32, name="q_col")

        def q_columns():
            bank = take("qt", [P, 2, P], BF16)
            for h in range(2):
                nc.tensor.transpose(bank[:, h, :], q_rows[:, h, :], ident_bf[:])
            nc.scalar.copy(out=q_col[:], in_=bank[:, :, 0:2 * GROUPS].rearrange("m h (g b) -> m g h b", b=2))
            give("qt")

        tiles = {}

        def new(name, unit, shape, dtype, bufs=1, align=32):
            tiles[(name, unit)] = work.tile(shape, dtype, name=name, bufs=bufs, align_bytes=align)
            return tiles[(name, unit)]

        def get(name, unit):
            return tiles[(name, unit)]

        def block(tile, b):
            return tile[:, b * P:(b + 1) * P]

        def flat(bank):
            return bank[:].rearrange("p b m -> p (b m)")

        def by_gate(ap):
            return ap.rearrange("p b (i o) -> p i b o", i=NI)

        def turn_sum(key, parts, plain_block):
            bank = take(key, [P, BLOCKS, P], F32)
            for b in range(BLOCKS):
                for index, part in enumerate(parts):
                    nc.tensor.matmul(bank[:, b, :], lhsT=block(part, b), rhs=ident[:], start=(index == 0), stop=(index == len(parts) - 1),
                                     is_transpose=not (b == plain_block and index == 0))

        def mu_mm(unit, j):
            bank = take(("mu", unit, j), [P, KP], F32)
            mx(bank[:], wq[(unit // GROUPS, "mu")], j * P, xq[unit % GROUPS], 0, KP, True, True)

        def residual(unit, j):
            r = new("r%d" % j, unit, [P, KP], F32, 3)
            nc.vector.tensor_tensor(out=r[:], in0=y_turned[unit // GROUPS][:, unit % GROUPS], in1=at(("mu", unit, j))[:], op=ALU.subtract)
            give(("mu", unit, j))

        def square(unit, j):
            z2 = new("z2%d" % j, unit, [P, KP], F32)
            nc.scalar.activation(out=z2[:], in_=get("r%d" % j, unit)[:], func=ACT.Square, scale=column(half_root, unit, j))

        def d_mm(unit, j):
            bank = take(("d", unit, j), [P, KP], F32)
            mx(bank[:], wq[(unit // GROUPS, "c")], j * P, xq[unit % GROUPS], 0, KP, True, False)
            mx(bank[:], wq[(unit // GROUPS, "c")], 0, xq[unit % GROUPS], 0, KP, False, True)

        def d1_copy(unit):
            nc.scalar.copy(out=new("d1", unit, [P, KP], F32)[:], in_=at(("d", unit, 1))[:])

        def max_12(unit):
            nc.vector.scalar_tensor_tensor(out=new("m12", unit, [P, KP], F32)[:], in0=at(("d", unit, 2))[:], scalar=0.0,
                                           in1=get("d1", unit)[:], op0=ALU.max, op1=ALU.max)

        def max_123(unit):
            nc.vector.tensor_tensor(out=new("gap", unit, [P, NJ, KP], F32)[:, 0], in0=at(("d", unit, 3))[:], in1=get("m12", unit)[:], op=ALU.max)

        def gap_j(unit, j):
            gap = get("gap", unit)
            nc.vector.tensor_tensor(out=gap[:, j], in0=gap[:, 0], in1=at(("d", unit, j))[:], op=ALU.subtract)
            give(("d", unit, j))

        def exp_gap(unit, half):
            eg = new("eg", unit, [P, NJ, KP], F32) if half == 0 else get("eg", unit)
            rows = slice(2 * half, 2 * half + 2)
            nc.scalar.activation(out=eg[:, rows], in_=get("gap", unit)[:, rows], func=ACT.Exp, scale=-1.0)

        def sum_s(unit):
            turn_sum(("S", unit), [get("eg", unit)[:, j] for j in range(NJ)], 2)

        def s_copy(unit):
            nc.scalar.copy(out=new("S", unit, [P, NI, BLOCKS, OC], F32)[:], in_=by_gate(at(("S", unit))[:]))
            give(("S", unit))

        def s_pairs(unit):
            return get("S", unit)[:].rearrange("p (i1 i0) b o -> p i1 i0 (b o)", i1=2)

        def pair(unit):
            nc.vector.tensor_tensor(out=new("pair", unit, [P, 2, P], F32)[:], in0=s_pairs(unit)[:, :, 0], in1=s_pairs(unit)[:, :, 1], op=ALU.mult)

        def cofactor(unit):
            other = get("pair", unit)[:, ::-1, :].unsqueeze(2).broadcast_to([P, 2, 2, P])
            nc.gpsimd.tensor_tensor(out=new("C", unit, [P, 2, 2, P], F32, 2)[:], in0=s_pairs(unit)[:, :, ::-1, :], in1=other, op=ALU.mult)

        def cofactors(unit):
            return get("C", unit)[:].rearrange("p i1 i0 (b o) -> p (i1 i0) b o", b=BLOCKS)

        def cost_mm(unit, j):
            turn_sum(("cost", unit, j), [get("gap", unit)[:, j], get("z2%d" % j, unit)], 0)

        def cost_copy(unit, j):
            nc.scalar.copy(out=new("cost%d" % j, unit, [P, KP], F32)[:], in_=flat(at(("cost", unit, j))))
            give(("cost", unit, j))

        def a_mm(unit):
            bank = take(("a", unit), [P, BLOCKS, P], F32)
            for b in range(BLOCKS):
                mx(bank[:, b, :], xq[unit % GROUPS], b * P, wq[(unit // GROUPS, "a")], 0, P, True, True)

        def min_pair(unit, half):
            least = new("least", unit, [P, 2, KP], F32) if half == 0 else get("least", unit)
            nc.vector.tensor_tensor(out=least[:, half], in0=get("cost%d" % (2 * half), unit)[:], in1=get("cost%d" % (2 * half + 1), unit)[:], op=ALU.min)

        def min_j(unit):
            least = get("least", unit)
            nc.vector.tensor_tensor(out=least[:, 0], in0=least[:, 0], in1=least[:, 1], op=ALU.min)

        def add_a(unit):
            least = get("least", unit)
            nc.vector.tensor_tensor(out=least[:, 1], in0=least[:, 0], in1=flat(at(("a", unit))), op=ALU.add)

        def min_i1(unit):
            gated = get("least", unit)[:, 1].rearrange("p (b i1 m) -> p b i1 m", b=BLOCKS, i1=2)
            nc.vector.tensor_tensor(out=new("low2", unit, [P, BLOCKS, 2 * OC], F32)[:], in0=gated[:, :, 0], in1=gated[:, :, 1], op=ALU.min)

        def min_i0(unit):
            low2 = get("low2", unit)
            nc.vector.tensor_tensor(out=new("low", unit, [P, BLOCKS, OC], F32)[:], in0=low2[:, :, 0:OC], in1=low2[:, :, OC:], op=ALU.min)

        def shift(unit):
            low = get("low", unit)[:].unsqueeze(2).broadcast_to([P, BLOCKS, NI, OC])
            nc.vector.tensor_tensor(out=new("shift", unit, [P, KP], F32)[:].rearrange("p (b i o) -> p b i o", b=BLOCKS, i=NI),
                                    in0=at(("a", unit))[:].rearrange("p b (i o) -> p b i o", i=NI), in1=low, op=ALU.subtract)
            give(("a", unit))

        def arg_mm(unit, j):
            turn_sum(("arg", unit, j), [get("cost%d" % j, unit), get("shift", unit)], None if j == 2 and unit < LAST else 0)

        def exp_arg(unit, j):
            nc.scalar.activation(out=new("e%d" % j, unit, [P, KP], F32)[:], in_=flat(at(("arg", unit, j))), func=ACT.Exp,
                                 scale=-1.0, bias=column(half_s, unit, j))
            give(("arg", unit, j))

        def product(unit, j):
            r = get("r%d" % j, unit)
            engine = nc.gpsimd if 0 < unit < LAST and j > 0 else nc.vector
            engine.tensor_tensor(out=r[:], in0=r[:], in1=get("e%d" % j, unit)[:], op=ALU.mult)

        def sum_e(unit):
            turn_sum(("E", unit), [get("e%d" % j, unit) for j in range(NJ)], 2)

        def weigh_sums(unit):
            nc.vector.tensor_tensor(out=new("EC", unit, [P, NI, BLOCKS, OC], F32)[:], in0=by_gate(at(("E", unit))[:]),
                                    in1=cofactors(unit), op=ALU.mult)
            give(("E", unit))

        def total_i1(unit):
            terms = get("EC", unit)[:].rearrange("p (i1 i0) b o -> p i1 (i0 b o)", i1=2)
            nc.vector.tensor_tensor(out=new("Z2", unit, [P, 2 * P], F32)[:], in0=terms[:, 0], in1=terms[:, 1], op=ALU.add)

        def total_i0(unit):
            z_two = get("Z2", unit)
            nc.vector.tensor_tensor(out=new("Z", unit, [P, P], F32)[:], in0=z_two[:, 0:P], in1=z_two[:, P:], op=ALU.add)

        def invert(unit):
            nc.vector.reciprocal(out=new("rz", unit, [P, P], F32)[:], in_=get("Z", unit)[:])

        def weigh_q(unit):
            q_spread = q_col[:, unit % GROUPS].rearrange("p h b -> p (h b)").unsqueeze(2).broadcast_to([P, BLOCKS, OC])
            nc.vector.tensor_tensor(out=new("rq", unit, [P, BLOCKS, OC], F32)[:], in0=get("rz", unit)[:].rearrange("p (b o) -> p b o", b=BLOCKS),
                                    in1=q_spread, op=ALU.mult)

        def factor(unit):
            rq = get("rq", unit)[:].unsqueeze(1).broadcast_to([P, NI, BLOCKS, OC])
            nc.vector.tensor_tensor(out=by_gate(new("f", unit, [P, BLOCKS, P], F32)[:]), in0=cofactors(unit), in1=rq, op=ALU.mult)

        def turn_factor(unit):
            bank = take(("ft", unit), [P, BLOCKS, P], F32)
            for b in range(BLOCKS):
                nc.tensor.transpose(bank[:, b, :], get("f", unit)[:, b, :], ident[:])

        def gradient(unit, j):
            nc.vector.scalar_tensor_tensor(out=new("gm%d" % j, unit, [P, KP], BF16)[:], in0=get("r%d" % j, unit)[:], scalar=column(var, unit, j),
                                           in1=flat(at(("ft", unit))), op0=ALU.mult, op1=ALU.mult)
            if j == NJ - 1:
                give(("ft", unit))

        def turn_gradient(unit, half):
            bank = take(("gt", unit, half), [P, 2, 2, P], F32)
            for j0 in range(2):
                words = get("gm%d" % (2 * half + j0), unit)[:].bitcast(F32)
                for h in range(2):
                    nc.tensor.transpose(bank[:, j0, h, :], block(words, h), ident[:])

        def copy_gradient(unit, half):
            gt = new("gt", unit, [P, 2, 2, P, 2], F32, 1, 64) if half == 0 else get("gt", unit)
            nc.scalar.copy(out=gt[:, half], in_=at(("gt", unit, half))[:].rearrange("p j0 h m -> p j0 m h"))
            give(("gt", unit, half))

        gq = {}

        def quantise_gm(unit):
            gq[unit] = quantise("gq", get("gt", unit)[:].rearrange("p j1 j0 m h -> p (j1 j0 m h)").bitcast(BF16), 4)

        def out_pass(chunk, n, group):
            bank = take(("out", chunk, n), [P, KP], F32) if group == 0 else at(("out", chunk, n))
            mx(bank[:], xuq[group], n * P, gq[chunk * GROUPS + group], 0, KP, group == 0, group == GROUPS - 1)

        def out_mm(chunk, n):
            for group in range(GROUPS):
                out_pass(chunk, n, group)

        def out_copy(on_vector, chunk, n):
            res = work.tile([P, EXPERTS, OC], F32, name="res", bufs=ROW_TILES)
            dst = res[:].rearrange("p (i j) o -> p i j o", i=NI)
            src = at(("out", chunk, n))[:].rearrange("p (j i o) -> p i j o", j=NJ, i=NI)
            if on_vector:
                nc.vector.tensor_scalar(out=dst, in0=src, scalar1=0.125, scalar2=None, op0=ALU.mult)
            else:
                nc.scalar.activation(out=dst, in_=src, func=ACT.Copy, scale=0.125)
            give(("out", chunk, n))
            queue = nc.scalar if on_vector else nc.sync
            queue.dma_start(out=out[n * P:(n + 1) * P].rearrange("d i j o -> d (i j) o")[:, :, chunk * OC:(chunk + 1) * OC], in_=res[:])

        nc.vector.tensor_scalar(out=wsn[:], in0=ws[:], scalar1=-1.0, scalar2=None, op0=ALU.mult)
        widen(ON_SCALAR, "mu", wb_mu[0][:, 1], ws, 1)
        widen(ON_VECTOR, "mu", wb_mu[0][:, 0], ws, 0)
        for h in range(2):
            turn_x(0, h)
        for h in range(2):
            copy_x(0, h)
        for t in (2, 3):
            widen(ON_VECTOR, "mu", wb_mu[1][:, t - 2], ws, t)
        for t in (0, 1):
            widen(ON_SCALAR, "c", wb_c[0][:, t], ws, t)
        gain_x(0)
        widen(ON_VECTOR, "c", wb_c[1][:, 0], ws, 2)
        quantise_xg(0)
        widen(ON_VECTOR, "c", wb_c[1][:, 1], ws, 3)
        spread_y(0)
        variance_columns()
        for h in range(2):
            turn_x(1, h)
        for h in range(2):
            copy_x(1, h)
        turn_y(0)
        for j in range(NJ):
            interleave(ON_VECTOR, 0, "c", j)
        interleave(ON_VECTOR, 0, "mu", 0)
        quantise_w(0, "c")
        for j in range(1, NJ):
            interleave(ON_VECTOR, 0, "mu", j)
        quantise_w(0, "mu")

        def next_chunk(unit):
            return unit // GROUPS + 1

        def next_kind(unit):
            return ("c", "mu")[unit % GROUPS]

        def next_weights(unit, j):
            if next_chunk(unit) < CHUNKS:
                interleave(j == NJ - 1, next_chunk(unit), next_kind(unit), j)

        def next_codes(unit):
            if next_chunk(unit) < CHUNKS:
                quantise_w(next_chunk(unit), next_kind(unit))

        def next_small_vector(unit):
            if next_chunk(unit) < CHUNKS:
                if unit % GROUPS == 0:
                    spread_y(next_chunk(unit))
                else:
                    quantise_w(next_chunk(unit), "a")

        def next_small_scalar(unit):
            if next_chunk(unit) < CHUNKS and unit % GROUPS == 0:
                interleave(ON_SCALAR, next_chunk(unit), "a", 0)
                turn_y(next_chunk(unit))
            if unit == 0:
                q_columns()

        def token_weights(unit, half):
            if unit < 2 * GROUPS:
                (weigh_x, interleave_x)[unit % 2](unit // 2, half)

        def token_codes(unit):
            if unit < 2 * GROUPS and unit % 2 == 1:
                quantise_xu(unit // 2)

        def first_gate_row(unit, t):
            if unit == 0:
                widen(ON_SCALAR, "a", wb_a[:, t], wsn, t)

        def head_rest(unit):
            if unit == 0:
                gain_x(1)
                interleave(ON_VECTOR, 0, "a", 0)
                quantise_xg(1)
                quantise_w(0, "a")
                nc.vector.tensor_copy(out=u32[:], in_=u_sb[:])

        def when(unit, step, *args):
            if 0 <= unit <= LAST:
                step(unit, *args)

        def out_tile(iteration, slot):
            chunk, later = divmod(iteration - (GROUPS + 2), GROUPS)
            return (chunk, 2 * later + slot) if 0 <= chunk < CHUNKS - 2 else None

        def out_product(iteration, slot):
            if out_tile(iteration, slot):
                out_mm(*out_tile(iteration, slot))

        def out_store(iteration, slot):
            if out_tile(iteration, slot):
                out_copy(ON_SCALAR, *out_tile(iteration, slot))

        for iteration in range(-1, UNITS):
            ahead, cur, mid, old = iteration + 1, iteration, iteration - 1, iteration - 2
            when(mid, shift)
            when(mid, arg_mm, 0)
            when(cur, residual, 0)
            when(cur, max_123)
            when(mid, exp_arg, 0)
            when(mid, arg_mm, 1)
            when(cur, square, 0)
            when(cur, first_gate_row, 0)
            when(cur, residual, 1)
            when(cur, gap_j, 1)
            when(mid, product, 0)
            when(mid, exp_arg, 1)
            when(cur, mu_mm, 2)
            when(cur, mu_mm, 3)
            when(mid, arg_mm, 2)
            when(cur, square, 1)
            when(cur, first_gate_row, 1)
            when(cur, residual, 2)
            when(cur, gap_j, 2)
            when(mid, product, 1)
            when(mid, exp_arg, 2)
            when(cur, cost_mm, 0)
            when(mid, arg_mm, 3)
            when(cur, square, 2)
            when(cur, first_gate_row, 2)
            when(cur, residual, 3)
            when(cur, gap_j, 3)
            when(mid, product, 2)
            when(cur, cost_copy, 0)
            when(mid, exp_arg, 3)
            when(cur, cost_mm, 1)
            when(cur, square, 3)
            when(cur, first_gate_row, 3)
            when(old, gradient, 0)
            when(old, gradient, 1)
            when(mid, product, 3)
            when(cur, cost_copy, 1)
            when(mid, sum_e)
            when(cur, exp_gap, 0)
            when(mid, token_weights, 1)
            when(old, gradient, 2)
            when(old, gradient, 3)
            when(cur, cost_mm, 2)
            when(old, turn_gradient, 0)
            when(cur, cost_copy, 2)
            when(cur, cost_mm, 3)
            when(old, copy_gradient, 0)
            when(old, turn_gradient, 1)
            when(cur, head_rest)
            when(cur, min_pair, 0)
            when(mid, token_codes)
            when(mid, weigh_sums)
            when(cur, next_weights, 3)
            when(mid, total_i1)
            when(cur, next_codes)
            when(mid, total_i0)
            when(cur, next_small_vector)
            when(cur, cost_copy, 3)
            when(old, copy_gradient, 1)
            when(cur, a_mm)
            when(ahead, d_mm, 1)
            when(cur, exp_gap, 1)
            out_product(iteration, 0)
            when(mid, invert)
            when(cur, min_pair, 1)
            when(mid, weigh_q)
            when(cur, min_j)
            when(mid, factor)
            when(cur, add_a)
            when(ahead, d1_copy)
            when(cur, token_weights, 0)
            when(cur, next_small_scalar)
            when(ahead, d_mm, 2)
            when(cur, sum_s)
            out_store(iteration, 0)
            when(cur, s_copy)
            out_product(iteration, 1)
            when(old, quantise_gm)
            when(cur, min_i1)
            when(ahead, max_12)
            when(cur, min_i0)
            when(ahead, next_weights, 0)
            when(ahead, next_weights, 1)
            when(mid, turn_factor)
            when(ahead, d_mm, 3)
            out_store(iteration, 1)
            when(ahead, mu_mm, 0)
            when(ahead, mu_mm, 1)
            when(ahead, next_weights, 2)
            when(cur, pair)
            when(cur, cofactor)

        mid, old = LAST, LAST - 1
        for n in range(2):
            out_mm(CHUNKS - 2, n)
        shift(mid)
        for half in range(2):
            arg_mm(mid, half)
            gradient(old, 2 * half)
            gradient(old, 2 * half + 1)
            exp_arg(mid, half)
        for j in range(2, NJ):
            arg_mm(mid, j)
            product(mid, j - 2)
            exp_arg(mid, j)
        for half in range(2):
            turn_gradient(old, half)
        product(mid, 2)
        sum_e(mid)
        for half in range(2):
            copy_gradient(old, half)
        for n in range(2):
            out_copy(ON_SCALAR, CHUNKS - 2, n)
        for n in range(2, ROW_TILES):
            out_mm(CHUNKS - 2, n)
            out_copy(ON_SCALAR, CHUNKS - 2, n)
        product(mid, 3)
        weigh_sums(mid)
        quantise_gm(old)
        total_i1(mid)
        for n in range(2):
            out_pass(CHUNKS - 1, n, 0)
        total_i0(mid)
        invert(mid)
        weigh_q(mid)
        factor(mid)
        turn_factor(mid)
        for half in range(2):
            gradient(mid, 2 * half)
            gradient(mid, 2 * half + 1)
            turn_gradient(mid, half)
            copy_gradient(mid, half)
        for n in range(2, ROW_TILES):
            out_pass(CHUNKS - 1, n, 0)
        quantise_gm(mid)
        for n in range(ROW_TILES):
            out_pass(CHUNKS - 1, n, GROUPS - 1)
        for n in range(ROW_TILES):
            out_copy(n % 2 == 1, CHUNKS - 1, n)
